import numpy as np
import ml_dtypes


def mxq(x, axis, fmt="e4m3"):
    dtype, down = {"e4m3": (ml_dtypes.float8_e4m3fn, 7), "e5m2": (ml_dtypes.float8_e5m2, 14)}[fmt]
    v = np.moveaxis(np.asarray(x, np.float32).astype(ml_dtypes.bfloat16).astype(np.float64), axis, -1)
    blocks = v.reshape(v.shape[:-1] + (-1, 32))
    amax = np.abs(blocks).max(-1, keepdims=True)
    byte = np.maximum(np.where(amax > 0, np.frexp(amax)[1] - 1 + 127, 0) - down, 1)
    scale = np.exp2(byte - 127.0)
    codes = (blocks / scale).astype(np.float32).astype(dtype).astype(np.float64)
    return np.moveaxis((codes * scale).reshape(v.shape), -1, axis)


WIDE = False


def mx_kscale(k):
    if not WIDE:
        return np.ones(k)
    levels = np.array([10, -10, 5, -5, 0])
    if k % 512:
        return np.exp2(np.random.permutation(np.resize(levels, k // 32))).repeat(32)
    a = np.empty((k // 512, 16))
    for p in range(k // 512):
        a[p, :8] = np.random.permutation(np.resize(levels, 8))
        for g in range(8):
            far = levels[np.abs(levels - a[p, g]) >= 10]
            a[p, g + 8] = far[np.random.randint(len(far))]
    return np.exp2(a.ravel()).repeat(32)


def f64(x):
    return np.asarray(x).astype(np.float64)


def striped(idx):
    return np.tile(idx.reshape(-1, 16).T, (8, 1)).astype(np.uint16)


def unstriped(offs):
    return offs[:16].T.reshape(-1).astype(np.int64)


E2M1 = np.array([0.0, 0.5, 1.0, 1.5, 2.0, 3.0, 4.0, 6.0, -0.0, -0.5, -1.0, -1.5, -2.0, -3.0, -4.0, -6.0])


def pack_weight(w, fmt):
    k, n = w.shape
    w = f64(np.asarray(w, np.float32).astype(ml_dtypes.bfloat16)).reshape(k // 32, 32, n)
    amax = np.abs(w).max(1)
    if fmt == "e4m3":
        byte = np.frexp(amax)[1] - 1 + 127 - 7
    else:
        mant, ex = np.frexp(amax / 6.0)
        byte = np.where(mant > 0.5, ex, ex - 1) + 127
    byte = np.clip(np.where(amax > 0, byte, 1), 1, 254)
    scaled = (w * np.exp2(127.0 - byte)[:, None, :]).reshape(k, n).astype(np.float32)
    by_word = np.ascontiguousarray(scaled.reshape(k // 512, 128, 4, n).transpose(0, 1, 3, 2))
    if fmt == "e4m3":
        words = by_word.astype(ml_dtypes.float8_e4m3fn).view(np.uint8)
    else:
        c = by_word.astype(ml_dtypes.float4_e2m1fn).view(np.uint8) & 0xF
        words = (c[..., 0::2] | (c[..., 1::2] << 4)).reshape(k // 512, 128, 2 * n)
    return np.ascontiguousarray(words), np.ascontiguousarray(byte.astype(np.uint8).reshape(k // 512, 16, n))


def unpack_weight(words, scales, fmt):
    g, _, n = scales.shape
    words = np.ascontiguousarray(words).reshape(g, 128, n, -1)
    if fmt == "e4m3":
        vals = words.view(ml_dtypes.float8_e4m3fn).astype(np.float64)
    else:
        nib = np.empty((g, 128, n, 4), np.uint8)
        nib[..., 0::2] = words & 0xF
        nib[..., 1::2] = words >> 4
        vals = E2M1[nib]
    vals = vals * np.repeat(np.exp2(scales.astype(np.float64) - 127.0), 8, axis=1)[..., None]
    return vals.transpose(0, 1, 3, 2).reshape(g * 512, n)


def gelu(v):
    return 0.5 * v * (1.0 + np.tanh(np.sqrt(2.0 / np.pi) * (v + 0.044715 * v**3)))


K, T, E, C, H, N = 512, 768, 8, 128, 512, 128
PAD = 32


def by_expert(wq, xq):
    return np.concatenate([wq[e].T @ xq[:, e * C:(e + 1) * C] for e in range(E)], axis=1)


def setup_inputs():
    n = np.random.standard_normal
    s = mx_kscale(K)[:, None]
    u = mx_kscale(H)
    first = np.random.permutation(np.repeat(np.arange(E), T // E))
    second = (first + 1 + np.random.permutation(np.repeat(np.arange(E - 1), -(-T // (E - 1)))[:T])) % E
    while np.bincount(second, minlength=E).max() != T // E:
        load = np.bincount(second, minlength=E); hi, lo = int(load.argmax()), int(load.argmin())
        t = np.flatnonzero((second == hi) & (first != lo))[0]; second[t] = lo
    slot_token = np.empty(E * C, np.int64); pos = np.empty((2, T), np.int64); fill = np.zeros(E, np.int64)
    place = np.stack([np.random.permutation(C) for _ in range(E)])
    for r, deal in enumerate((first, second)):
        for t in np.random.permutation(T):
            e = deal[t]
            if fill[e] < C: j = e * C + place[e, fill[e]]; fill[e] += 1; slot_token[j] = t; pos[r, t] = j
            else: pos[r, t] = E * C + t % PAD
    g = np.random.uniform(0.2, 0.8, T)
    w1 = [pack_weight(m, "e2m1") for m in n((E, K, H)) / np.sqrt(K) / s[None]]
    w3 = [pack_weight(m, "e2m1") for m in n((E, K, H)) / np.sqrt(K) / s[None] * u[None, None, :]]
    w2 = [pack_weight(m, "e2m1") for m in n((E, H, N)) / np.sqrt(H) / u[None, :, None]]
    return {
        "xT": (n((K, T)) * s).astype(np.float32),
        "w1_words": np.stack([m[0] for m in w1]),
        "w1_scales": np.stack([m[1] for m in w1]),
        "w3_words": np.stack([m[0] for m in w3]),
        "w3_scales": np.stack([m[1] for m in w3]),
        "w2_words": np.stack([m[0] for m in w2]),
        "w2_scales": np.stack([m[1] for m in w2]),
        "gate": np.stack([np.tile(g, (N, 1)), np.tile(1.0 - g, (N, 1))]).astype(np.float32),
        "offs": striped(slot_token),
        "pos1": striped(pos[0]),
        "pos2": striped(pos[1]),
    }


def reference(xT, w1_words, w1_scales, w3_words, w3_scales, w2_words, w2_scales, gate, offs, pos1, pos2):
    idx = unstriped(offs)
    w1 = np.stack([unpack_weight(w1_words[e], w1_scales[e], "e2m1") for e in range(E)])
    w3 = np.stack([unpack_weight(w3_words[e], w3_scales[e], "e2m1") for e in range(E)])
    w2 = np.stack([unpack_weight(w2_words[e], w2_scales[e], "e2m1") for e in range(E)])
    xq = mxq(f64(xT)[:, idx], 0, "e4m3")
    h = gelu(by_expert(w1, xq))
    h = h * by_expert(w3, xq)
    y = by_expert(w2, mxq(h, 0, "e4m3"))
    y = np.concatenate([y, np.zeros((N, PAD))], axis=1)
    return f64(gate[0]) * y[:, unstriped(pos1)] + f64(gate[1]) * y[:, unstriped(pos2)]

@@ -1,0 +1,257 @@
+from contextlib import ExitStack
+
+import concourse.mybir as mybir
+from concourse.masks import make_identity
+
+K, T, E, C, H, N = 512, 768, 8, 128, 512, 128
+PAD = 32
+P = 128
+S = E * C
+WARM_PASSES = 10
+GPSIMD_EXPERTS = ()
+FLOPS = 2 * S * (2 * K * H + H * N)
+
+F32 = mybir.dt.float32
+BF16 = mybir.dt.bfloat16
+I32 = mybir.dt.int32
+U32 = mybir.dt.uint32
+U16 = mybir.dt.uint16
+U8 = mybir.dt.uint8
+FP8X4 = mybir.dt.float8_e4m3fn_x4
+FP4X4 = mybir.dt.float4_e2m1fn_x4
+GELU = mybir.ActivationFunctionType.Gelu_apprx_tanh
+MULT = mybir.AluOpType.mult
+ADD = mybir.AluOpType.add
+
+X_CHUNKS = (256, 256, 256)
+X_BLOCKS = ((256,), (256,), (128, 128))
+
+
+def tile_moe_cap2_glu_gelu_kernel(
+    tc, xT, w1_words, w1_scales, w3_words, w3_scales, w2_words, w2_scales, gate, offs, pos1, pos2, out
+):
+    nc = tc.nc
+    with ExitStack() as ctx:
+        held = ctx.enter_context(tc.tile_pool(name="held", bufs=1))
+        ring = ctx.enter_context(tc.tile_pool(name="ring", bufs=3))
+        pair = ctx.enter_context(tc.tile_pool(name="pair", bufs=2))
+        psum = ctx.enter_context(tc.psum_pool(name="psum", bufs=2))
+
+        offs_t = held.tile([P, S // 16], U16, name="offs_t")
+        pos1_t = held.tile([P, T // 16], U16, name="pos1_t")
+        pos2_t = held.tile([P, T // 16], U16, name="pos2_t")
+
+        warm = held.tile([P, 1], F32, name="warm")
+        s1 = held.tile([P, E, H], U8, name="s1", align_bytes=64)
+        s3 = held.tile([P, E, H], U8, name="s3", align_bytes=64)
+        s2 = held.tile([P, E, N], U8, name="s2", align_bytes=64)
+        xs = held.tile([P, T], U8, name="xs", align_bytes=64)
+        w2t = held.tile([P, E, 2 * N], U8, name="w2t", align_bytes=64)
+        words, raw, gates = [], [], []
+        for g in range(E // 2):
+            w = held.tile([P, 2, 2, 2 * H], U8, name=f"words{g}", align_bytes=64)
+            words.append(w)
+        for c, width in enumerate(X_CHUNKS):
+            r = held.tile([P, 4, width], F32, name=f"raw{c}")
+            raw.append(r)
+        for i in range(2):
+            g_t = held.tile([P, T], F32, name=f"gate{i}")
+            gates.append(g_t)
+
+        def zero(bytes_3d):
+            nc.vector.memset(bytes_3d.rearrange("p e n -> p (e n)").bitcast(I32), 0)
+
+        nc.vector.memset(warm[:], 0.0)
+        nc.scalar.activation(warm[:], warm[:], GELU)
+        zero(s1[:])
+        zero(s3[:])
+        nc.vector.memset(xs[:].bitcast(I32), 0)
+        zero(s2[:])
+        idle = held.tile([P, 4 * P], BF16, name="idle", align_bytes=64)
+        idle_q = held.tile([P, P], U32, name="idle_q", align_bytes=64)
+        idle_s = held.tile([P, P], U8, name="idle_s", align_bytes=64)
+        nc.vector.memset(idle[:], 0.0)
+        nc.vector.quantize_mx(out=idle_q[:].bitcast(FP8X4), scales=idle_s[:], in_=idle[:])
+        ident = held.tile([P, P], F32, name="ident")
+        make_identity(nc, ident[:])
+        y = held.tile([P, S + PAD], F32, name="y")
+        nc.gpsimd.memset(y[:, S:], 0.0)
+
+        def load_x(c):
+            t0 = sum(X_CHUNKS[:c])
+            nc.sync.dma_start(
+                out=raw[c][:], in_=xT.rearrange("(p j) w -> p j w", j=4)[:, :, t0 : t0 + X_CHUNKS[c]]
+            )
+
+        def load_scales(plane, scales):
+            for r in range(4):
+                nc.sync.dma_start(
+                    out=plane[r:P:32].bitcast(I32),
+                    in_=scales.bitcast(I32).rearrange("e s (q r) n -> r q (e s) n", r=4)[r],
+                )
+
+        def load_words(g):
+            for i, hbm in enumerate((w1_words, w3_words)):
+                nc.sync.dma_start(
+                    out=words[g][:, i].bitcast(I32),
+                    in_=hbm.bitcast(I32)[2 * g : 2 * g + 2].rearrange("e s p n -> p (e s) n"),
+                )
+
+        for c in range(len(X_CHUNKS)):
+            load_x(c)
+        nc.sync.dma_start(offs_t[:], offs)
+        load_scales(s1, w1_scales)
+        load_words(0)
+        load_scales(s3, w3_scales)
+        load_words(1)
+        nc.sync.dma_start(out=w2t[:].bitcast(I32), in_=w2_words.bitcast(I32).rearrange("e s p n -> p (e s) n"))
+        load_scales(s2, w2_scales)
+        load_words(2)
+        load_words(3)
+        nc.sync.dma_start(pos1_t[:], pos1)
+        nc.sync.dma_start(pos2_t[:], pos2)
+        for i in range(2):
+            nc.sync.dma_start(out=gates[i][:], in_=gate[i])
+
+        idle_p = psum.tile([P, P], F32, name="yp")
+        for i in range(WARM_PASSES):
+            nc.tensor.matmul_mx(
+                out=idle_p[:],
+                lhsT=s1[:, 0, : 2 * P].bitcast(FP4X4),
+                lhsT_scale=s1[:, 1, :P],
+                rhs=idle_q[:].bitcast(FP8X4),
+                rhs_scale=idle_s[:],
+                start=True,
+                stop=True,
+            )
+
+        xq = held.tile([P, T], U32, name="xq", align_bytes=64)
+        t0 = 0
+        for c, widths in enumerate(X_BLOCKS):
+            xb = held.tile([P, X_CHUNKS[c], 4], BF16, name=f"xb{c}", align_bytes=64)
+            lo = 0
+            for width in widths:
+                hi, cut = lo + width, lo + width * 21 // 128 * 4
+                src = raw[c][:].rearrange("p j w -> p w j")
+                nc.vector.tensor_copy(out=xb[:, lo:cut], in_=src[:, lo:cut])
+                nc.scalar.copy(out=xb[:, cut:hi], in_=src[:, cut:hi])
+                lo = hi
+            lo = 0
+            for width in widths:
+                cols = slice(t0, t0 + width)
+                nc.vector.quantize_mx(
+                    out=xq[:, cols].bitcast(FP8X4),
+                    scales=xs[:, cols],
+                    in_=xb[:, lo : lo + width].rearrange("p w j -> p (w j)"),
+                )
+                lo, t0 = lo + width, t0 + width
+
+        gq, gs = {}, {}
+
+        def gather(e0, n):
+            if e0 % 2 == 0:
+                gq[e0 // 2] = pair.tile([P, 2 * C], U32, name="gq", align_bytes=64)
+                gs[e0 // 2] = pair.tile([P, 2 * C], U8, name="gs", align_bytes=64)
+            sl = slice(e0 % 2 * C, (e0 % 2 + n) * C)
+            lst = offs_t[:, e0 * C // 16 : (e0 + n) * C // 16]
+            nc.vector.tensor_copy(gq[e0 // 2][:, sl], xq[:].indirect(lst))
+            nc.vector.tensor_copy(gs[e0 // 2][:, sl], xs[:].indirect(lst))
+
+        a_t, b_t, h_t, xt_t, hq_t, hs_t, y_t, g_t2, hi_t = {}, {}, {}, {}, {}, {}, {}, {}, {}
+
+        def first(e):
+            sl = slice(e % 2 * C, (e % 2 + 1) * C)
+            for i, (d, plane, nm) in enumerate(((a_t, s1, "a"), (b_t, s3, "b"))):
+                d[e] = psum.tile([P, H], F32, name=nm)
+                nc.tensor.matmul_mx(
+                    out=d[e][:],
+                    lhsT=gq[e // 2][:, sl].bitcast(FP8X4),
+                    lhsT_scale=gs[e // 2][:, sl],
+                    rhs=words[e // 2][:, i, e % 2].bitcast(FP4X4),
+                    rhs_scale=plane[:, e],
+                    start=True,
+                    stop=True,
+                )
+
+        def gelu(e):
+            g_t2[e] = ring.tile([P, 2, P, 2], F32, name="g")
+            nc.scalar.activation(g_t2[e][:], a_t[e][:].rearrange("s (p u w) -> s u p w", u=2, w=2), GELU)
+
+        def mul(e):
+            h_t[e] = ring.tile([P, 2, P, 2], BF16, name="h")
+            b = b_t[e][:].rearrange("s (p u w) -> s u p w", u=2, w=2)
+            if e in GPSIMD_EXPERTS:
+                bs = ring.tile([P, 2, P, 2], F32, name="bs")
+                nc.scalar.copy(bs[:], b)
+                for u in range(2):
+                    nc.gpsimd.tensor_tensor(h_t[e][:, u], bs[:, u], g_t2[e][:, u], MULT)
+            elif e == E - 1:
+                for u in range(2):
+                    nc.vector.tensor_tensor(h_t[e][:, u], b[:, u], g_t2[e][:, u], MULT)
+            else:
+                nc.vector.tensor_tensor(h_t[e][:], b, g_t2[e][:], MULT)
+
+        def turn(e):
+            xt_t[e] = psum.tile([P, 2, P], F32, name="xt")
+            pairs = h_t[e][:].rearrange("s u p w -> s (u p w)").bitcast(F32)
+            for u in range(2):
+                nc.tensor.transpose(xt_t[e][:, u], pairs[:, u * P : (u + 1) * P], ident[:])
+
+        def lay(e):
+            hi_t[e] = ring.tile([P, C, 4], BF16, name="hi", align_bytes=64)
+            dst = hi_t[e][:].rearrange("p s d -> p (s d)").bitcast(F32).rearrange("p (s u) -> p s u", u=2)
+            srcv = xt_t[e][:].rearrange("p u s -> p s u")
+            nc.scalar.copy(dst, srcv)
+
+        def quant(e):
+            hq_t[e] = ring.tile([P, C], U32, name="hq", align_bytes=64)
+            hs_t[e] = ring.tile([P, C], U8, name="hs", align_bytes=64)
+            nc.vector.quantize_mx(out=hq_t[e][:].bitcast(FP8X4), scales=hs_t[e][:], in_=hi_t[e][:].rearrange("p s d -> p (s d)"))
+
+        def second(e):
+            y_t[e] = psum.tile([P, C], F32, name="yp")
+            nc.tensor.matmul_mx(
+                out=y_t[e][:],
+                lhsT=w2t[:, e].bitcast(FP4X4),
+                lhsT_scale=s2[:, e],
+                rhs=hq_t[e][:].bitcast(FP8X4),
+                rhs_scale=hs_t[e][:],
+                start=True,
+                stop=True,
+            )
+
+        def keep(e):
+            nc.scalar.copy(y[:, e * C : (e + 1) * C], y_t[e][:])
+
+        groups = [(0, 1), (1, 1), (2, 2), (4, 2), (6, 2)]
+        gather(*groups.pop(0))
+        gather(*groups.pop(0))
+        first(0)
+        for e in range(E + 2):
+            if groups and groups[0][0] <= e + 2:
+                gather(*groups.pop(0))
+            if e < E:
+                gelu(e)
+                mul(e)
+                turn(e)
+            if 0 <= e - 1 < E:
+                lay(e - 1)
+                quant(e - 1)
+                second(e - 1)
+            if 0 <= e - 2 < E:
+                keep(e - 2)
+            if e + 1 < E:
+                first(e + 1)
+
+        o1 = held.tile([P, T], F32, name="o1")
+        o2 = held.tile([P, T], F32, name="o2")
+        res = held.tile([P, T], F32, name="res")
+        parts = ((0, 512), (512, T))
+        for lo, hi in parts:
+            sl, ls = slice(lo, hi), slice(lo // 16, hi // 16)
+            nc.vector.tensor_tensor(o1[:, sl], y[:].indirect(pos1_t[:, ls]), gates[0][:, sl], MULT)
+            nc.vector.tensor_tensor(o2[:, sl], y[:].indirect(pos2_t[:, ls]), gates[1][:, sl], MULT)
+        for lo, hi in parts:
+            sl = slice(lo, hi)
+            nc.vector.tensor_tensor(res[:, sl], o1[:, sl], o2[:, sl], ADD)
+            nc.sync.dma_start(out=out[:, sl], in_=res[:, sl])

@@ -7,8 +7,6 @@ K, T, E, C, H, N = 512, 768, 8, 128, 512, 128
 PAD = 32
 P = 128
 S = E * C
-WARM_PASSES = 10
-GPSIMD_EXPERTS = ()
 FLOPS = 2 * S * (2 * K * H + H * N)
 
 F32 = mybir.dt.float32
@@ -23,8 +21,11 @@ GELU = mybir.ActivationFunctionType.Gelu_apprx_tanh
 MULT = mybir.AluOpType.mult
 ADD = mybir.AluOpType.add
 
-X_CHUNKS = (256, 256, 256)
-X_BLOCKS = ((256,), (256,), (128, 128))
+X_BLOCKS = (((256, 168), (128, 84)), ((256, 168),), ((128, 64),))
+SCALE_GROUPS = ((0, 2), (2, 5), (5, 8))
+QUANT_GROUPS = ((0, 2), (2, 3), (3, 7), (7, 8))
+KEEP_GROUPS = ((0, 3), (3, 7), (7, 8))
+OUT_PARTS = ((0, 384), (384, 640), (640, T))
 
 
 def tile_moe_cap2_glu_gelu_kernel(
@@ -33,111 +34,100 @@ def tile_moe_cap2_glu_gelu_kernel(
     nc = tc.nc
     with ExitStack() as ctx:
         held = ctx.enter_context(tc.tile_pool(name="held", bufs=1))
-        ring = ctx.enter_context(tc.tile_pool(name="ring", bufs=3))
-        pair = ctx.enter_context(tc.tile_pool(name="pair", bufs=2))
-        psum = ctx.enter_context(tc.psum_pool(name="psum", bufs=2))
+        ring = ctx.enter_context(tc.tile_pool(name="ring", bufs=4))
+        psum1 = ctx.enter_context(tc.psum_pool(name="psum1", bufs=1))
+        psum2 = ctx.enter_context(tc.psum_pool(name="psum2", bufs=2))
+        psum3 = ctx.enter_context(tc.psum_pool(name="psum3", bufs=3))
 
         offs_t = held.tile([P, S // 16], U16, name="offs_t")
         pos1_t = held.tile([P, T // 16], U16, name="pos1_t")
         pos2_t = held.tile([P, T // 16], U16, name="pos2_t")
 
-        warm = held.tile([P, 1], F32, name="warm")
-        s1 = held.tile([P, E, H], U8, name="s1", align_bytes=64)
-        s3 = held.tile([P, E, H], U8, name="s3", align_bytes=64)
-        s2 = held.tile([P, E, N], U8, name="s2", align_bytes=64)
-        xs = held.tile([P, T], U8, name="xs", align_bytes=64)
-        w2t = held.tile([P, E, 2 * N], U8, name="w2t", align_bytes=64)
-        words, raw, gates = [], [], []
-        for g in range(E // 2):
-            w = held.tile([P, 2, 2, 2 * H], U8, name=f"words{g}", align_bytes=64)
-            words.append(w)
-        for c, width in enumerate(X_CHUNKS):
-            r = held.tile([P, 4, width], F32, name=f"raw{c}")
-            raw.append(r)
-        for i in range(2):
-            g_t = held.tile([P, T], F32, name=f"gate{i}")
-            gates.append(g_t)
+        def zero(tile_3d):
+            nc.vector.memset(tile_3d.rearrange("p e n -> p (e n)").bitcast(I32), 0)
 
-        def zero(bytes_3d):
-            nc.vector.memset(bytes_3d.rearrange("p e n -> p (e n)").bitcast(I32), 0)
-
-        nc.vector.memset(warm[:], 0.0)
-        nc.scalar.activation(warm[:], warm[:], GELU)
-        zero(s1[:])
-        zero(s3[:])
-        nc.vector.memset(xs[:].bitcast(I32), 0)
-        zero(s2[:])
-        idle = held.tile([P, 4 * P], BF16, name="idle", align_bytes=64)
-        idle_q = held.tile([P, P], U32, name="idle_q", align_bytes=64)
-        idle_s = held.tile([P, P], U8, name="idle_s", align_bytes=64)
-        nc.vector.memset(idle[:], 0.0)
-        nc.vector.quantize_mx(out=idle_q[:].bitcast(FP8X4), scales=idle_s[:], in_=idle[:])
+        y = held.tile([P, S + PAD], F32, name="y")
+        zeros = held.tile([P, PAD], F32, name="zeros")
+        nc.gpsimd.memset(zeros[:], 0.0)
+        nc.scalar.activation(y[:, S:], zeros[:], GELU)
         ident = held.tile([P, P], F32, name="ident")
         make_identity(nc, ident[:])
-        y = held.tile([P, S + PAD], F32, name="y")
-        nc.gpsimd.memset(y[:, S:], 0.0)
+
+        planes = {}
+        for g, (e0, e1) in enumerate(SCALE_GROUPS):
+            for i in range(2):
+                planes[i, g] = held.tile([P, e1 - e0, H], U8, name=f"plane{i}_{g}", align_bytes=64)
+                zero(planes[i, g][:])
+        s2 = held.tile([P, E, N], U8, name="s2", align_bytes=64)
+        xs = held.tile([P, T], U8, name="xs", align_bytes=64)
+        zero(s2[:])
+        nc.vector.memset(xs[:].bitcast(I32), 0)
+        w2t = held.tile([P, E, 2 * N], U8, name="w2t", align_bytes=64)
+        words = {}
+        for g in range(E // 2):
+            for i in range(2):
+                words[i, g] = held.tile([P, 2, 2 * H], U8, name=f"words{i}_{g}", align_bytes=64)
+        widths = [sum(w for w, v in blocks) for blocks in X_BLOCKS]
+        raw = [held.tile([P, 4, w], F32, name=f"raw{c}") for c, w in enumerate(widths)]
+        gates = [held.tile([P, T], F32, name=f"gate{i}") for i in range(2)]
 
         def load_x(c):
-            t0 = sum(X_CHUNKS[:c])
-            nc.sync.dma_start(
-                out=raw[c][:], in_=xT.rearrange("(p j) w -> p j w", j=4)[:, :, t0 : t0 + X_CHUNKS[c]]
-            )
+            t0 = sum(widths[:c])
+            nc.sync.dma_start(out=raw[c][:], in_=xT.rearrange("(p j) w -> p j w", j=4)[:, :, t0 : t0 + widths[c]])
 
-        def load_scales(plane, scales):
+        def load_scales(plane, scales, e0, e1):
             for r in range(4):
                 nc.sync.dma_start(
                     out=plane[r:P:32].bitcast(I32),
-                    in_=scales.bitcast(I32).rearrange("e s (q r) n -> r q (e s) n", r=4)[r],
+                    in_=scales.bitcast(I32)[e0:e1].rearrange("e s (q r) n -> r q (e s) n", r=4)[r],
                 )
 
-        def load_words(g):
-            for i, hbm in enumerate((w1_words, w3_words)):
-                nc.sync.dma_start(
-                    out=words[g][:, i].bitcast(I32),
-                    in_=hbm.bitcast(I32)[2 * g : 2 * g + 2].rearrange("e s p n -> p (e s) n"),
-                )
+        def load_plane(i, g):
+            load_scales(planes[i, g], (w1_scales, w3_scales)[i], *SCALE_GROUPS[g])
 
-        for c in range(len(X_CHUNKS)):
-            load_x(c)
+        def load_words(i, g):
+            nc.sync.dma_start(
+                out=words[i, g][:].bitcast(I32),
+                in_=(w1_words, w3_words)[i].bitcast(I32)[2 * g : 2 * g + 2].rearrange("e s p n -> p (e s) n"),
+            )
+
+        load_x(0)
         nc.sync.dma_start(offs_t[:], offs)
-        load_scales(s1, w1_scales)
-        load_words(0)
-        load_scales(s3, w3_scales)
-        load_words(1)
+        load_x(1)
+        load_x(2)
+        load_plane(0, 0)
+        load_words(0, 0)
+        load_words(1, 0)
+        load_plane(1, 0)
+        load_words(0, 1)
+        load_plane(0, 1)
+        load_words(1, 1)
+        load_plane(1, 1)
+        load_words(0, 2)
+        load_words(1, 2)
+        load_plane(0, 2)
         nc.sync.dma_start(out=w2t[:].bitcast(I32), in_=w2_words.bitcast(I32).rearrange("e s p n -> p (e s) n"))
-        load_scales(s2, w2_scales)
-        load_words(2)
-        load_words(3)
+        load_plane(1, 2)
+        load_words(0, 3)
+        load_scales(s2, w2_scales, 0, E)
+        load_words(1, 3)
         nc.sync.dma_start(pos1_t[:], pos1)
         nc.sync.dma_start(pos2_t[:], pos2)
         for i in range(2):
             nc.sync.dma_start(out=gates[i][:], in_=gate[i])
 
-        idle_p = psum.tile([P, P], F32, name="yp")
-        for i in range(WARM_PASSES):
-            nc.tensor.matmul_mx(
-                out=idle_p[:],
-                lhsT=s1[:, 0, : 2 * P].bitcast(FP4X4),
-                lhsT_scale=s1[:, 1, :P],
-                rhs=idle_q[:].bitcast(FP8X4),
-                rhs_scale=idle_s[:],
-                start=True,
-                stop=True,
-            )
-
         xq = held.tile([P, T], U32, name="xq", align_bytes=64)
         t0 = 0
-        for c, widths in enumerate(X_BLOCKS):
-            xb = held.tile([P, X_CHUNKS[c], 4], BF16, name=f"xb{c}", align_bytes=64)
+        for c, blocks in enumerate(X_BLOCKS):
+            xb = held.tile([P, widths[c], 4], BF16, name=f"xb{c}", align_bytes=64)
+            src = raw[c][:].rearrange("p j w -> p w j")
             lo = 0
-            for width in widths:
-                hi, cut = lo + width, lo + width * 21 // 128 * 4
-                src = raw[c][:].rearrange("p j w -> p w j")
-                nc.vector.tensor_copy(out=xb[:, lo:cut], in_=src[:, lo:cut])
-                nc.scalar.copy(out=xb[:, cut:hi], in_=src[:, cut:hi])
-                lo = hi
+            for width, on_vector in blocks:
+                nc.vector.tensor_copy(out=xb[:, lo : lo + on_vector], in_=src[:, lo : lo + on_vector])
+                nc.scalar.copy(out=xb[:, lo + on_vector : lo + width], in_=src[:, lo + on_vector : lo + width])
+                lo = lo + width
             lo = 0
-            for width in widths:
+            for width, on_vector in blocks:
                 cols = slice(t0, t0 + width)
                 nc.vector.quantize_mx(
                     out=xq[:, cols].bitcast(FP8X4),
@@ -146,112 +136,135 @@ def tile_moe_cap2_glu_gelu_kernel(
                 )
                 lo, t0 = lo + width, t0 + width
 
-        gq, gs = {}, {}
+        gq, gs, a_t, b_t, g_t, h_t, xt_t, hi_t, hq_t, hs_t, y_t = [{} for i in range(11)]
 
-        def gather(e0, n):
-            if e0 % 2 == 0:
-                gq[e0 // 2] = pair.tile([P, 2 * C], U32, name="gq", align_bytes=64)
-                gs[e0 // 2] = pair.tile([P, 2 * C], U8, name="gs", align_bytes=64)
-            sl = slice(e0 % 2 * C, (e0 % 2 + n) * C)
-            lst = offs_t[:, e0 * C // 16 : (e0 + n) * C // 16]
-            nc.vector.tensor_copy(gq[e0 // 2][:, sl], xq[:].indirect(lst))
-            nc.vector.tensor_copy(gs[e0 // 2][:, sl], xs[:].indirect(lst))
+        def group_of(groups, e):
+            return [g for g, (e0, e1) in enumerate(groups) if e0 <= e < e1][0]
 
-        a_t, b_t, h_t, xt_t, hq_t, hs_t, y_t, g_t2, hi_t = {}, {}, {}, {}, {}, {}, {}, {}, {}
+        def gather(e):
+            gq[e] = ring.tile([P, C], U32, name="gq", align_bytes=64)
+            gs[e] = ring.tile([P, C], U8, name="gs", align_bytes=64)
+            lst = offs_t[:, e * C // 16 : (e + 1) * C // 16]
+            nc.vector.tensor_copy(gq[e][:], xq[:].indirect(lst))
+            nc.vector.tensor_copy(gs[e][:], xs[:].indirect(lst))
 
         def first(e):
-            sl = slice(e % 2 * C, (e % 2 + 1) * C)
-            for i, (d, plane, nm) in enumerate(((a_t, s1, "a"), (b_t, s3, "b"))):
-                d[e] = psum.tile([P, H], F32, name=nm)
+            g = group_of(SCALE_GROUPS, e)
+            a_t[e] = psum2.tile([P, H], F32, name="a")
+            b_t[e] = psum3.tile([P, H], F32, name="b")
+            for i, acc in enumerate((a_t[e], b_t[e])):
                 nc.tensor.matmul_mx(
-                    out=d[e][:],
-                    lhsT=gq[e // 2][:, sl].bitcast(FP8X4),
-                    lhsT_scale=gs[e // 2][:, sl],
-                    rhs=words[e // 2][:, i, e % 2].bitcast(FP4X4),
-                    rhs_scale=plane[:, e],
+                    out=acc[:],
+                    lhsT=gq[e][:].bitcast(FP8X4),
+                    lhsT_scale=gs[e][:],
+                    rhs=words[i, e // 2][:, e % 2].bitcast(FP4X4),
+                    rhs_scale=planes[i, g][:, e - SCALE_GROUPS[g][0]],
                     start=True,
                     stop=True,
                 )
 
         def gelu(e):
-            g_t2[e] = ring.tile([P, 2, P, 2], F32, name="g")
-            nc.scalar.activation(g_t2[e][:], a_t[e][:].rearrange("s (p u w) -> s u p w", u=2, w=2), GELU)
+            g_t[e] = ring.tile([P, 2, P, 2], F32, name="g")
+            nc.scalar.activation(g_t[e][:], a_t[e][:].rearrange("s (p u w) -> s u p w", u=2, w=2), GELU)
 
         def mul(e):
             h_t[e] = ring.tile([P, 2, P, 2], BF16, name="h")
             b = b_t[e][:].rearrange("s (p u w) -> s u p w", u=2, w=2)
-            if e in GPSIMD_EXPERTS:
-                bs = ring.tile([P, 2, P, 2], F32, name="bs")
-                nc.scalar.copy(bs[:], b)
+            if e == E - 1:
                 for u in range(2):
-                    nc.gpsimd.tensor_tensor(h_t[e][:, u], bs[:, u], g_t2[e][:, u], MULT)
-            elif e == E - 1:
-                for u in range(2):
-                    nc.vector.tensor_tensor(h_t[e][:, u], b[:, u], g_t2[e][:, u], MULT)
+                    nc.vector.tensor_tensor(h_t[e][:, u], b[:, u], g_t[e][:, u], MULT)
             else:
-                nc.vector.tensor_tensor(h_t[e][:], b, g_t2[e][:], MULT)
+                nc.vector.tensor_tensor(h_t[e][:], b, g_t[e][:], MULT)
 
         def turn(e):
-            xt_t[e] = psum.tile([P, 2, P], F32, name="xt")
+            xt_t[e] = psum2.tile([P, 2, P], F32, name="xt")
             pairs = h_t[e][:].rearrange("s u p w -> s (u p w)").bitcast(F32)
             for u in range(2):
                 nc.tensor.transpose(xt_t[e][:, u], pairs[:, u * P : (u + 1) * P], ident[:])
 
         def lay(e):
-            hi_t[e] = ring.tile([P, C, 4], BF16, name="hi", align_bytes=64)
-            dst = hi_t[e][:].rearrange("p s d -> p (s d)").bitcast(F32).rearrange("p (s u) -> p s u", u=2)
-            srcv = xt_t[e][:].rearrange("p u s -> p s u")
-            nc.scalar.copy(dst, srcv)
+            g = group_of(QUANT_GROUPS, e)
+            e0, e1 = QUANT_GROUPS[g]
+            if e == e0:
+                hi_t[g] = held.tile([P, (e1 - e0) * C * 4], BF16, name=f"hi{g}", align_bytes=64)
+            mine = hi_t[g][:, (e - e0) * C * 4 : (e - e0 + 1) * C * 4]
+            nc.scalar.copy(mine.bitcast(F32).rearrange("p (s u) -> p s u", u=2), xt_t[e][:].rearrange("p u s -> p s u"))
 
-        def quant(e):
-            hq_t[e] = ring.tile([P, C], U32, name="hq", align_bytes=64)
-            hs_t[e] = ring.tile([P, C], U8, name="hs", align_bytes=64)
-            nc.vector.quantize_mx(out=hq_t[e][:].bitcast(FP8X4), scales=hs_t[e][:], in_=hi_t[e][:].rearrange("p s d -> p (s d)"))
+        def quant(g):
+            e0, e1 = QUANT_GROUPS[g]
+            hq_t[g] = held.tile([P, (e1 - e0) * C], U32, name=f"hq{g}", align_bytes=64)
+            hs_t[g] = held.tile([P, (e1 - e0) * C], U8, name=f"hs{g}", align_bytes=64)
+            nc.vector.quantize_mx(out=hq_t[g][:].bitcast(FP8X4), scales=hs_t[g][:], in_=hi_t[g][:])
 
         def second(e):
-            y_t[e] = psum.tile([P, C], F32, name="yp")
+            g, k = group_of(QUANT_GROUPS, e), group_of(KEEP_GROUPS, e)
+            k0, k1 = KEEP_GROUPS[k]
+            if e == k0:
+                if e == E - 1:
+                    y_t[k] = psum1.tile([P, C], F32, name="yp")
+                else:
+                    y_t[k] = psum2.tile([P, (k1 - k0) * C], F32, name="a")
+            cols = slice((e - QUANT_GROUPS[g][0]) * C, (e - QUANT_GROUPS[g][0] + 1) * C)
             nc.tensor.matmul_mx(
-                out=y_t[e][:],
+                out=y_t[k][:, (e - k0) * C : (e - k0 + 1) * C],
                 lhsT=w2t[:, e].bitcast(FP4X4),
                 lhsT_scale=s2[:, e],
-                rhs=hq_t[e][:].bitcast(FP8X4),
-                rhs_scale=hs_t[e][:],
+                rhs=hq_t[g][:, cols].bitcast(FP8X4),
+                rhs_scale=hs_t[g][:, cols],
                 start=True,
                 stop=True,
             )
 
-        def keep(e):
-            nc.scalar.copy(y[:, e * C : (e + 1) * C], y_t[e][:])
+        def keep(k):
+            k0, k1 = KEEP_GROUPS[k]
+            if k == 1:
+                nc.vector.tensor_copy(y[:, k0 * C : k1 * C], y_t[k][:])
+            else:
+                nc.scalar.copy(y[:, k0 * C : k1 * C], y_t[k][:])
 
-        groups = [(0, 1), (1, 1), (2, 2), (4, 2), (6, 2)]
-        gather(*groups.pop(0))
-        gather(*groups.pop(0))
-        first(0)
-        for e in range(E + 2):
-            if groups and groups[0][0] <= e + 2:
-                gather(*groups.pop(0))
-            if e < E:
-                gelu(e)
-                mul(e)
-                turn(e)
-            if 0 <= e - 1 < E:
-                lay(e - 1)
-                quant(e - 1)
-                second(e - 1)
-            if 0 <= e - 2 < E:
-                keep(e - 2)
-            if e + 1 < E:
-                first(e + 1)
+        for e in range(4):
+            gather(e)
+        for e in range(3):
+            first(e)
+            gelu(e)
+        for e in range(E):
+            mul(e)
+            turn(e)
+            lay(e)
+            if e + 4 < E:
+                gather(e + 4)
+            if e + 3 < E:
+                first(e + 3)
+                gelu(e + 3)
+            for g, (e0, e1) in enumerate(QUANT_GROUPS):
+                if min(e1, E - 1) == e:
+                    quant(g)
+                    if e == E - 1:
+                        for d in range(e0, e1):
+                            second(d)
+            if e + 3 == E - 1:
+                for d in range(*KEEP_GROUPS[0]):
+                    second(d)
+                keep(0)
+        keep(1)
+        keep(2)
 
         o1 = held.tile([P, T], F32, name="o1")
         o2 = held.tile([P, T], F32, name="o2")
         res = held.tile([P, T], F32, name="res")
-        parts = ((0, 512), (512, T))
-        for lo, hi in parts:
-            sl, ls = slice(lo, hi), slice(lo // 16, hi // 16)
-            nc.vector.tensor_tensor(o1[:, sl], y[:].indirect(pos1_t[:, ls]), gates[0][:, sl], MULT)
-            nc.vector.tensor_tensor(o2[:, sl], y[:].indirect(pos2_t[:, ls]), gates[1][:, sl], MULT)
-        for lo, hi in parts:
-            sl = slice(lo, hi)
-            nc.vector.tensor_tensor(res[:, sl], o1[:, sl], o2[:, sl], ADD)
-            nc.sync.dma_start(out=out[:, sl], in_=res[:, sl])
+
+        def pick(o, pos_t, gate_t, part):
+            lo, hi = part
+            nc.vector.tensor_tensor(o[:, lo:hi], y[:].indirect(pos_t[:, lo // 16 : hi // 16]), gate_t[:, lo:hi], MULT)
+
+        def finish(part):
+            lo, hi = part
+            nc.vector.tensor_tensor(res[:, lo:hi], o1[:, lo:hi], o2[:, lo:hi], ADD)
+            nc.sync.dma_start(out=out[:, lo:hi], in_=res[:, lo:hi])
+
+        for n, part in enumerate(OUT_PARTS):
+            pick(o1, pos1_t, gates[0], part)
+            if n > 0:
+                finish(OUT_PARTS[n - 1])
+            pick(o2, pos2_t, gates[1], part)
+        finish(OUT_PARTS[-1])

@@ -22,9 +22,10 @@ MULT = mybir.AluOpType.mult
 ADD = mybir.AluOpType.add
 
 X_BLOCKS = (((256, 168), (128, 84)), ((256, 168),), ((128, 64),))
-SCALE_GROUPS = ((0, 2), (2, 5), (5, 8))
-QUANT_GROUPS = ((0, 2), (2, 3), (3, 7), (7, 8))
-KEEP_GROUPS = ((0, 3), (3, 7), (7, 8))
+SCALE_GROUPS = ((0, 2), (2, 8))
+QUANT_GROUPS = ((0, 2), (2, 4), (4, 6), (6, 7), (7, 8))
+KEEP_GROUPS = ((0, 2), (2, 6), (6, 7), (7, 8))
+KEEP_BANKS = ("y0", "b0", "y1", "y0")
 OUT_PARTS = ((0, 384), (384, 640), (640, T))
 
 
@@ -35,9 +36,7 @@ def tile_moe_cap2_glu_gelu_kernel(
     with ExitStack() as ctx:
         held = ctx.enter_context(tc.tile_pool(name="held", bufs=1))
         ring = ctx.enter_context(tc.tile_pool(name="ring", bufs=4))
-        psum1 = ctx.enter_context(tc.psum_pool(name="psum1", bufs=1))
-        psum2 = ctx.enter_context(tc.psum_pool(name="psum2", bufs=2))
-        psum3 = ctx.enter_context(tc.psum_pool(name="psum3", bufs=3))
+        psum = ctx.enter_context(tc.psum_pool(name="psum", bufs=1))
 
         offs_t = held.tile([P, S // 16], U16, name="offs_t")
         pos1_t = held.tile([P, T // 16], U16, name="pos1_t")
@@ -69,7 +68,7 @@ def tile_moe_cap2_glu_gelu_kernel(
                 words[i, g] = held.tile([P, 2, 2 * H], U8, name=f"words{i}_{g}", align_bytes=64)
         widths = [sum(w for w, v in blocks) for blocks in X_BLOCKS]
         raw = [held.tile([P, 4, w], F32, name=f"raw{c}") for c, w in enumerate(widths)]
-        gates = [held.tile([P, T], F32, name=f"gate{i}") for i in range(2)]
+        gates = held.tile([P, 2, T], F32, name="gates")
 
         def load_x(c):
             t0 = sum(widths[:c])
@@ -105,16 +104,13 @@ def tile_moe_cap2_glu_gelu_kernel(
         load_plane(1, 1)
         load_words(0, 2)
         load_words(1, 2)
-        load_plane(0, 2)
         nc.sync.dma_start(out=w2t[:].bitcast(I32), in_=w2_words.bitcast(I32).rearrange("e s p n -> p (e s) n"))
-        load_plane(1, 2)
-        load_words(0, 3)
         load_scales(s2, w2_scales, 0, E)
+        load_words(0, 3)
         load_words(1, 3)
         nc.sync.dma_start(pos1_t[:], pos1)
         nc.sync.dma_start(pos2_t[:], pos2)
-        for i in range(2):
-            nc.sync.dma_start(out=gates[i][:], in_=gate[i])
+        nc.sync.dma_start(out=gates[:], in_=gate.rearrange("i p t -> p i t"))
 
         xq = held.tile([P, T], U32, name="xq", align_bytes=64)
         t0 = 0
@@ -150,8 +146,8 @@ def tile_moe_cap2_glu_gelu_kernel(
 
         def first(e):
             g = group_of(SCALE_GROUPS, e)
-            a_t[e] = psum2.tile([P, H], F32, name="a")
-            b_t[e] = psum3.tile([P, H], F32, name="b")
+            a_t[e] = psum.tile([P, H], F32, name=f"a{e % 3}")
+            b_t[e] = psum.tile([P, H], F32, name=f"b{e % 3}")
             for i, acc in enumerate((a_t[e], b_t[e])):
                 nc.tensor.matmul_mx(
                     out=acc[:],
@@ -177,7 +173,7 @@ def tile_moe_cap2_glu_gelu_kernel(
                 nc.vector.tensor_tensor(h_t[e][:], b, g_t[e][:], MULT)
 
         def turn(e):
-            xt_t[e] = psum2.tile([P, 2, P], F32, name="xt")
+            xt_t[e] = psum.tile([P, 2, P], F32, name=f"a{(e + 2) % 3}")
             pairs = h_t[e][:].rearrange("s u p w -> s (u p w)").bitcast(F32)
             for u in range(2):
                 nc.tensor.transpose(xt_t[e][:, u], pairs[:, u * P : (u + 1) * P], ident[:])
@@ -200,10 +196,7 @@ def tile_moe_cap2_glu_gelu_kernel(
             g, k = group_of(QUANT_GROUPS, e), group_of(KEEP_GROUPS, e)
             k0, k1 = KEEP_GROUPS[k]
             if e == k0:
-                if e == E - 1:
-                    y_t[k] = psum1.tile([P, C], F32, name="yp")
-                else:
-                    y_t[k] = psum2.tile([P, (k1 - k0) * C], F32, name="a")
+                y_t[k] = psum.tile([P, (k1 - k0) * C], F32, name=KEEP_BANKS[k])
             cols = slice((e - QUANT_GROUPS[g][0]) * C, (e - QUANT_GROUPS[g][0] + 1) * C)
             nc.tensor.matmul_mx(
                 out=y_t[k][:, (e - k0) * C : (e - k0 + 1) * C],
@@ -229,25 +222,24 @@ def tile_moe_cap2_glu_gelu_kernel(
             gelu(e)
         for e in range(E):
             mul(e)
-            turn(e)
-            lay(e)
             if e + 4 < E:
                 gather(e + 4)
             if e + 3 < E:
                 first(e + 3)
                 gelu(e + 3)
+            turn(e)
+            lay(e)
             for g, (e0, e1) in enumerate(QUANT_GROUPS):
-                if min(e1, E - 1) == e:
+                if e1 == e + 1:
                     quant(g)
-                    if e == E - 1:
-                        for d in range(e0, e1):
-                            second(d)
-            if e + 3 == E - 1:
-                for d in range(*KEEP_GROUPS[0]):
-                    second(d)
+            if e == 1:
+                second(0)
+                second(1)
                 keep(0)
-        keep(1)
-        keep(2)
+        for e in range(2, E):
+            second(e)
+        for k in range(1, len(KEEP_GROUPS)):
+            keep(k)
 
         o1 = held.tile([P, T], F32, name="o1")
         o2 = held.tile([P, T], F32, name="o2")
@@ -263,8 +255,8 @@ def tile_moe_cap2_glu_gelu_kernel(
             nc.sync.dma_start(out=out[:, lo:hi], in_=res[:, lo:hi])
 
         for n, part in enumerate(OUT_PARTS):
-            pick(o1, pos1_t, gates[0], part)
+            pick(o1, pos1_t, gates[:, 0], part)
             if n > 0:
                 finish(OUT_PARTS[n - 1])
-            pick(o2, pos2_t, gates[1], part)
+            pick(o2, pos2_t, gates[:, 1], part)
         finish(OUT_PARTS[-1])

@@ -21,11 +21,14 @@ GELU = mybir.ActivationFunctionType.Gelu_apprx_tanh
 MULT = mybir.AluOpType.mult
 ADD = mybir.AluOpType.add
 
-X_BLOCKS = (((256, 168), (128, 84)), ((256, 168),), ((128, 64),))
-SCALE_GROUPS = ((0, 2), (2, 8))
-QUANT_GROUPS = ((0, 2), (2, 4), (4, 6), (6, 7), (7, 8))
+X_BLOCKS = (((256, 128), (128, 64)), ((256, 160),), ((128, 64),))
+SCALE_GROUPS = ((0, 4), (4, 8))
+QUANT_GROUPS = ((0, 2), (2, 6), (6, 7), (7, 8))
 KEEP_GROUPS = ((0, 2), (2, 6), (6, 7), (7, 8))
-KEEP_BANKS = ("y0", "b0", "y1", "y0")
+KEEP_BANKS = ("y0", "b0", "b2", "b1")
+TURN_BANKS = ("a3", "a0", "a1", "a2", "a0", "a1", "a2", "a3")
+CODE_BYTES = ("gq0", "gq1", "gq2", "gq3", "gq0", "gq3", "words1_1", "h0")
+SCALE_BYTES = ("gs0", "gs1", "gs2", "gs3", "gs0", "gs3", "plane1_0", "h1")
 OUT_PARTS = ((0, 384), (384, 640), (640, T))
 
 
@@ -35,7 +38,6 @@ def tile_moe_cap2_glu_gelu_kernel(
     nc = tc.nc
     with ExitStack() as ctx:
         held = ctx.enter_context(tc.tile_pool(name="held", bufs=1))
-        ring = ctx.enter_context(tc.tile_pool(name="ring", bufs=4))
         psum = ctx.enter_context(tc.psum_pool(name="psum", bufs=1))
 
         offs_t = held.tile([P, S // 16], U16, name="offs_t")
@@ -99,15 +101,15 @@ def tile_moe_cap2_glu_gelu_kernel(
         load_words(1, 0)
         load_plane(1, 0)
         load_words(0, 1)
-        load_plane(0, 1)
         load_words(1, 1)
         load_plane(1, 1)
-        load_words(0, 2)
         load_words(1, 2)
+        load_plane(0, 1)
+        load_words(0, 2)
+        load_words(1, 3)
+        load_words(0, 3)
         nc.sync.dma_start(out=w2t[:].bitcast(I32), in_=w2_words.bitcast(I32).rearrange("e s p n -> p (e s) n"))
         load_scales(s2, w2_scales, 0, E)
-        load_words(0, 3)
-        load_words(1, 3)
         nc.sync.dma_start(pos1_t[:], pos1)
         nc.sync.dma_start(pos2_t[:], pos2)
         nc.sync.dma_start(out=gates[:], in_=gate.rearrange("i p t -> p i t"))
@@ -138,15 +140,15 @@ def tile_moe_cap2_glu_gelu_kernel(
             return [g for g, (e0, e1) in enumerate(groups) if e0 <= e < e1][0]
 
         def gather(e):
-            gq[e] = ring.tile([P, C], U32, name="gq", align_bytes=64)
-            gs[e] = ring.tile([P, C], U8, name="gs", align_bytes=64)
+            gq[e] = held.tile([P, C], U32, name=CODE_BYTES[e], align_bytes=64)
+            gs[e] = held.tile([P, C], U8, name=SCALE_BYTES[e], align_bytes=64)
             lst = offs_t[:, e * C // 16 : (e + 1) * C // 16]
             nc.vector.tensor_copy(gq[e][:], xq[:].indirect(lst))
             nc.vector.tensor_copy(gs[e][:], xs[:].indirect(lst))
 
         def first(e):
             g = group_of(SCALE_GROUPS, e)
-            a_t[e] = psum.tile([P, H], F32, name=f"a{e % 3}")
+            a_t[e] = psum.tile([P, H], F32, name=f"a{e % 4}")
             b_t[e] = psum.tile([P, H], F32, name=f"b{e % 3}")
             for i, acc in enumerate((a_t[e], b_t[e])):
                 nc.tensor.matmul_mx(
@@ -160,11 +162,11 @@ def tile_moe_cap2_glu_gelu_kernel(
                 )
 
         def gelu(e):
-            g_t[e] = ring.tile([P, 2, P, 2], F32, name="g")
+            g_t[e] = held.tile([P, 2, P, 2], F32, name=f"g{e % 4}", align_bytes=64)
             nc.scalar.activation(g_t[e][:], a_t[e][:].rearrange("s (p u w) -> s u p w", u=2, w=2), GELU)
 
         def mul(e):
-            h_t[e] = ring.tile([P, 2, P, 2], BF16, name="h")
+            h_t[e] = held.tile([P, 2, P, 2], BF16, name=f"h{e}", align_bytes=64)
             b = b_t[e][:].rearrange("s (p u w) -> s u p w", u=2, w=2)
             if e == E - 1:
                 for u in range(2):
@@ -173,7 +175,7 @@ def tile_moe_cap2_glu_gelu_kernel(
                 nc.vector.tensor_tensor(h_t[e][:], b, g_t[e][:], MULT)
 
         def turn(e):
-            xt_t[e] = psum.tile([P, 2, P], F32, name=f"a{(e + 2) % 3}")
+            xt_t[e] = psum.tile([P, 2, P], F32, name=TURN_BANKS[e])
             pairs = h_t[e][:].rearrange("s u p w -> s (u p w)").bitcast(F32)
             for u in range(2):
                 nc.tensor.transpose(xt_t[e][:, u], pairs[:, u * P : (u + 1) * P], ident[:])
@@ -188,7 +190,7 @@ def tile_moe_cap2_glu_gelu_kernel(
 
         def quant(g):
             e0, e1 = QUANT_GROUPS[g]
-            hq_t[g] = held.tile([P, (e1 - e0) * C], U32, name=f"hq{g}", align_bytes=64)
+            hq_t[g] = held.tile([P, (e1 - e0) * C], U32, name="g3" if g == 1 else f"hq{g}", align_bytes=64)
             hs_t[g] = held.tile([P, (e1 - e0) * C], U8, name=f"hs{g}", align_bytes=64)
             nc.vector.quantize_mx(out=hq_t[g][:].bitcast(FP8X4), scales=hs_t[g][:], in_=hi_t[g][:])
 
@@ -220,22 +222,25 @@ def tile_moe_cap2_glu_gelu_kernel(
         for e in range(3):
             first(e)
             gelu(e)
+        gather(4)
         for e in range(E):
             mul(e)
-            if e + 4 < E:
-                gather(e + 4)
             if e + 3 < E:
                 first(e + 3)
                 gelu(e + 3)
             turn(e)
             lay(e)
+            if 0 < e < 4:
+                gather(e + 4)
             for g, (e0, e1) in enumerate(QUANT_GROUPS):
-                if e1 == e + 1:
+                if e1 == e + 1 == 2:
                     quant(g)
             if e == 1:
                 second(0)
                 second(1)
                 keep(0)
+        for g in range(1, len(QUANT_GROUPS)):
+            quant(g)
         for e in range(2, E):
             second(e)
         for k in range(1, len(KEEP_GROUPS)):

@@ -23,12 +23,11 @@ ADD = mybir.AluOpType.add
 
 X_BLOCKS = (((256, 128), (128, 64)), ((256, 160),), ((128, 64),))
 SCALE_GROUPS = ((0, 4), (4, 8))
-QUANT_GROUPS = ((0, 2), (2, 6), (6, 7), (7, 8))
-KEEP_GROUPS = ((0, 2), (2, 6), (6, 7), (7, 8))
-KEEP_BANKS = ("y0", "b0", "b2", "b1")
-TURN_BANKS = ("a3", "a0", "a1", "a2", "a0", "a1", "a2", "a3")
-CODE_BYTES = ("gq0", "gq1", "gq2", "gq3", "gq0", "gq3", "words1_1", "h0")
-SCALE_BYTES = ("gs0", "gs1", "gs2", "gs3", "gs0", "gs3", "plane1_0", "h1")
+QUANT_GROUPS = ((0, 2), (2, 4), (4, 6), (6, 7), (7, 8))
+KEEP_GROUPS = ((0, 4), (4, 7), (7, 8))
+KEEP_BANKS = ("b2", "b0", "y0")
+GATHER_GROUPS = ((0, 1), (1, 2), (2, 4), (4, 6), (6, 8))
+GATHER_TILES = (0, 1, 2, 3, 2)
 OUT_PARTS = ((0, 384), (384, 640), (640, T))
 
 
@@ -103,11 +102,11 @@ def tile_moe_cap2_glu_gelu_kernel(
         load_words(0, 1)
         load_words(1, 1)
         load_plane(1, 1)
-        load_words(1, 2)
         load_plane(0, 1)
         load_words(0, 2)
-        load_words(1, 3)
+        load_words(1, 2)
         load_words(0, 3)
+        load_words(1, 3)
         nc.sync.dma_start(out=w2t[:].bitcast(I32), in_=w2_words.bitcast(I32).rearrange("e s p n -> p (e s) n"))
         load_scales(s2, w2_scales, 0, E)
         nc.sync.dma_start(pos1_t[:], pos1)
@@ -139,30 +138,31 @@ def tile_moe_cap2_glu_gelu_kernel(
         def group_of(groups, e):
             return [g for g, (e0, e1) in enumerate(groups) if e0 <= e < e1][0]
 
-        def gather(e):
-            gq[e] = held.tile([P, C], U32, name=CODE_BYTES[e], align_bytes=64)
-            gs[e] = held.tile([P, C], U8, name=SCALE_BYTES[e], align_bytes=64)
-            lst = offs_t[:, e * C // 16 : (e + 1) * C // 16]
-            nc.vector.tensor_copy(gq[e][:], xq[:].indirect(lst))
-            nc.vector.tensor_copy(gs[e][:], xs[:].indirect(lst))
+        def gather(g):
+            e0, e1 = GATHER_GROUPS[g]
+            gq[g] = held.tile([P, (e1 - e0) * C], U32, name=f"gq{GATHER_TILES[g]}", align_bytes=64)
+            gs[g] = held.tile([P, (e1 - e0) * C], U8, name=f"gs{GATHER_TILES[g]}", align_bytes=64)
+            lst = offs_t[:, e0 * C // 16 : e1 * C // 16]
+            nc.vector.tensor_copy(gq[g][:], xq[:].indirect(lst))
+            nc.vector.tensor_copy(gs[g][:], xs[:].indirect(lst))
 
-        def first(e):
-            g = group_of(SCALE_GROUPS, e)
-            a_t[e] = psum.tile([P, H], F32, name=f"a{e % 4}")
-            b_t[e] = psum.tile([P, H], F32, name=f"b{e % 3}")
-            for i, acc in enumerate((a_t[e], b_t[e])):
-                nc.tensor.matmul_mx(
-                    out=acc[:],
-                    lhsT=gq[e][:].bitcast(FP8X4),
-                    lhsT_scale=gs[e][:],
-                    rhs=words[i, e // 2][:, e % 2].bitcast(FP4X4),
-                    rhs_scale=planes[i, g][:, e - SCALE_GROUPS[g][0]],
-                    start=True,
-                    stop=True,
-                )
+        def first(i, e):
+            g, s = group_of(GATHER_GROUPS, e), group_of(SCALE_GROUPS, e)
+            slots = slice((e - GATHER_GROUPS[g][0]) * C, (e - GATHER_GROUPS[g][0] + 1) * C)
+            acc = psum.tile([P, H], F32, name=(f"a{e % 4}", f"b{e % 3}")[i])
+            (a_t, b_t)[i][e] = acc
+            nc.tensor.matmul_mx(
+                out=acc[:],
+                lhsT=gq[g][:, slots].bitcast(FP8X4),
+                lhsT_scale=gs[g][:, slots],
+                rhs=words[i, e // 2][:, e % 2].bitcast(FP4X4),
+                rhs_scale=planes[i, s][:, e - SCALE_GROUPS[s][0]],
+                start=True,
+                stop=True,
+            )
 
         def gelu(e):
-            g_t[e] = held.tile([P, 2, P, 2], F32, name=f"g{e % 4}", align_bytes=64)
+            g_t[e] = held.tile([P, 2, P, 2], F32, name=f"g{e}", align_bytes=64)
             nc.scalar.activation(g_t[e][:], a_t[e][:].rearrange("s (p u w) -> s u p w", u=2, w=2), GELU)
 
         def mul(e):
@@ -175,7 +175,7 @@ def tile_moe_cap2_glu_gelu_kernel(
                 nc.vector.tensor_tensor(h_t[e][:], b, g_t[e][:], MULT)
 
         def turn(e):
-            xt_t[e] = psum.tile([P, 2, P], F32, name=TURN_BANKS[e])
+            xt_t[e] = psum.tile([P, 2, P], F32, name=f"a{(e + 2) % 4}")
             pairs = h_t[e][:].rearrange("s u p w -> s (u p w)").bitcast(F32)
             for u in range(2):
                 nc.tensor.transpose(xt_t[e][:, u], pairs[:, u * P : (u + 1) * P], ident[:])
@@ -190,7 +190,7 @@ def tile_moe_cap2_glu_gelu_kernel(
 
         def quant(g):
             e0, e1 = QUANT_GROUPS[g]
-            hq_t[g] = held.tile([P, (e1 - e0) * C], U32, name="g3" if g == 1 else f"hq{g}", align_bytes=64)
+            hq_t[g] = held.tile([P, (e1 - e0) * C], U32, name=f"hq{g}", align_bytes=64)
             hs_t[g] = held.tile([P, (e1 - e0) * C], U8, name=f"hs{g}", align_bytes=64)
             nc.vector.quantize_mx(out=hq_t[g][:].bitcast(FP8X4), scales=hs_t[g][:], in_=hi_t[g][:])
 
@@ -217,33 +217,30 @@ def tile_moe_cap2_glu_gelu_kernel(
             else:
                 nc.scalar.copy(y[:, k0 * C : k1 * C], y_t[k][:])
 
+        for g in range(4):
+            gather(g)
         for e in range(4):
-            gather(e)
-        for e in range(3):
-            first(e)
+            first(0, e)
+            if e < 3:
+                first(1, e)
             gelu(e)
-        gather(4)
         for e in range(E):
             mul(e)
             if e + 3 < E:
-                first(e + 3)
-                gelu(e + 3)
+                first(1, e + 3)
+            if e == 0:
+                gather(4)
             turn(e)
             lay(e)
-            if 0 < e < 4:
-                gather(e + 4)
+            if e + 4 < E:
+                first(0, e + 4)
+                gelu(e + 4)
             for g, (e0, e1) in enumerate(QUANT_GROUPS):
-                if e1 == e + 1 == 2:
+                if e1 == e + 1:
                     quant(g)
-            if e == 1:
-                second(0)
-                second(1)
-                keep(0)
-        for g in range(1, len(QUANT_GROUPS)):
-            quant(g)
-        for e in range(2, E):
+        for e in range(E):
             second(e)
-        for k in range(1, len(KEEP_GROUPS)):
+        for k in range(len(KEEP_GROUPS)):
             keep(k)
 
         o1 = held.tile([P, T], F32, name="o1")

@@ -21,7 +21,7 @@ GELU = mybir.ActivationFunctionType.Gelu_apprx_tanh
 MULT = mybir.AluOpType.mult
 ADD = mybir.AluOpType.add
 
-X_BLOCKS = (((256, 128), (128, 64)), ((256, 160),), ((128, 64),))
+X_BLOCKS = (((256, 128), (256, 128)), ((128, 80), (128, 80)))
 SCALE_GROUPS = ((0, 4), (4, 8))
 QUANT_GROUPS = ((0, 2), (2, 4), (4, 6), (6, 7), (7, 8))
 KEEP_GROUPS = ((0, 4), (4, 7), (7, 8))
@@ -92,9 +92,8 @@ def tile_moe_cap2_glu_gelu_kernel(
             )
 
         load_x(0)
-        nc.sync.dma_start(offs_t[:], offs)
         load_x(1)
-        load_x(2)
+        nc.sync.dma_start(offs_t[:], offs)
         load_plane(0, 0)
         load_words(0, 0)
         load_words(1, 0)

@@ -21,11 +21,11 @@ GELU = mybir.ActivationFunctionType.Gelu_apprx_tanh
 MULT = mybir.AluOpType.mult
 ADD = mybir.AluOpType.add
 
-X_BLOCKS = (((256, 128), (256, 128)), ((128, 80), (128, 80)))
+X_BLOCKS = (((256, 160), (256, 160)), ((128, 96), (128, 64)))
 SCALE_GROUPS = ((0, 4), (4, 8))
 QUANT_GROUPS = ((0, 2), (2, 4), (4, 6), (6, 7), (7, 8))
 KEEP_GROUPS = ((0, 4), (4, 7), (7, 8))
-KEEP_BANKS = ("b2", "b0", "y0")
+KEEP_BANKS = ("a0", "a3", "y0")
 GATHER_GROUPS = ((0, 1), (1, 2), (2, 4), (4, 6), (6, 8))
 GATHER_TILES = (0, 1, 2, 3, 2)
 OUT_PARTS = ((0, 384), (384, 640), (640, T))
@@ -116,11 +116,13 @@ def tile_moe_cap2_glu_gelu_kernel(
         t0 = 0
         for c, blocks in enumerate(X_BLOCKS):
             xb = held.tile([P, widths[c], 4], BF16, name=f"xb{c}", align_bytes=64)
-            src = raw[c][:].rearrange("p j w -> p w j")
+            src = raw[c][:].rearrange("p j (q i) -> p q j i", i=4)
+            dst = xb[:].rearrange("p (q i) j -> p q j i", i=4)
             lo = 0
             for width, on_vector in blocks:
-                nc.vector.tensor_copy(out=xb[:, lo : lo + on_vector], in_=src[:, lo : lo + on_vector])
-                nc.scalar.copy(out=xb[:, lo + on_vector : lo + width], in_=src[:, lo + on_vector : lo + width])
+                q0, q1, q2 = lo // 4, (lo + on_vector) // 4, (lo + width) // 4
+                nc.vector.tensor_copy(out=dst[:, q0:q1], in_=src[:, q0:q1])
+                nc.scalar.copy(out=dst[:, q1:q2], in_=src[:, q1:q2])
                 lo = lo + width
             lo = 0
             for width, on_vector in blocks:
@@ -174,7 +176,7 @@ def tile_moe_cap2_glu_gelu_kernel(
                 nc.vector.tensor_tensor(h_t[e][:], b, g_t[e][:], MULT)
 
         def turn(e):
-            xt_t[e] = psum.tile([P, 2, P], F32, name=f"a{(e + 2) % 4}")
+            xt_t[e] = psum.tile([P, 2, P], F32, name=f"a{(e + 2) % 4}" if e + 3 < E else f"b{e % 3}")
             pairs = h_t[e][:].rearrange("s u p w -> s (u p w)").bitcast(F32)
             for u in range(2):
                 nc.tensor.transpose(xt_t[e][:, u], pairs[:, u * P : (u + 1) * P], ident[:])
@@ -189,7 +191,7 @@ def tile_moe_cap2_glu_gelu_kernel(
 
         def quant(g):
             e0, e1 = QUANT_GROUPS[g]
-            hq_t[g] = held.tile([P, (e1 - e0) * C], U32, name=f"hq{g}", align_bytes=64)
+            hq_t[g] = held.tile([P, (e1 - e0) * C], U32, name=f"g{E - 1}" if g == 1 else f"hq{g}", align_bytes=64)
             hs_t[g] = held.tile([P, (e1 - e0) * C], U8, name=f"hs{g}", align_bytes=64)
             nc.vector.quantize_mx(out=hq_t[g][:].bitcast(FP8X4), scales=hs_t[g][:], in_=hi_t[g][:])
 
@@ -229,14 +231,15 @@ def tile_moe_cap2_glu_gelu_kernel(
                 first(1, e + 3)
             if e == 0:
                 gather(4)
-            turn(e)
-            lay(e)
             if e + 4 < E:
                 first(0, e + 4)
                 gelu(e + 4)
-            for g, (e0, e1) in enumerate(QUANT_GROUPS):
-                if e1 == e + 1:
-                    quant(g)
+            turn(e)
+            lay(e)
+            if e == 1:
+                quant(0)
+        for g in range(1, len(QUANT_GROUPS)):
+            quant(g)
         for e in range(E):
             second(e)
         for k in range(len(KEEP_GROUPS)):

@@ -25,10 +25,10 @@ X_BLOCKS = (((256, 160), (256, 160)), ((128, 96), (128, 64)))
 SCALE_GROUPS = ((0, 4), (4, 8))
 QUANT_GROUPS = ((0, 2), (2, 4), (4, 6), (6, 7), (7, 8))
 KEEP_GROUPS = ((0, 4), (4, 7), (7, 8))
-KEEP_BANKS = ("a0", "a3", "y0")
+KEEP_BANKS = ("a3", "a1", "y0")
 GATHER_GROUPS = ((0, 1), (1, 2), (2, 4), (4, 6), (6, 8))
 GATHER_TILES = (0, 1, 2, 3, 2)
-OUT_PARTS = ((0, 384), (384, 640), (640, T))
+OUT_PARTS = ((0, 512), (512, 640), (640, T))
 
 
 def tile_moe_cap2_glu_gelu_kernel(
@@ -175,8 +175,13 @@ def tile_moe_cap2_glu_gelu_kernel(
             else:
                 nc.vector.tensor_tensor(h_t[e][:], b, g_t[e][:], MULT)
 
+        def turn_bank(e):
+            if e < 4:
+                return f"a{(e + 2 + e // 2) % 4}"
+            return f"a{e % 4}" if e + 3 < E else f"b{e % 3}"
+
         def turn(e):
-            xt_t[e] = psum.tile([P, 2, P], F32, name=f"a{(e + 2) % 4}" if e + 3 < E else f"b{e % 3}")
+            xt_t[e] = psum.tile([P, 2, P], F32, name=turn_bank(e))
             pairs = h_t[e][:].rearrange("s u p w -> s (u p w)").bitcast(F32)
             for u in range(2):
                 nc.tensor.transpose(xt_t[e][:, u], pairs[:, u * P : (u + 1) * P], ident[:])
@@ -253,14 +258,18 @@ def tile_moe_cap2_glu_gelu_kernel(
             lo, hi = part
             nc.vector.tensor_tensor(o[:, lo:hi], y[:].indirect(pos_t[:, lo // 16 : hi // 16]), gate_t[:, lo:hi], MULT)
 
-        def finish(part):
+        def finish(part, queue):
             lo, hi = part
             nc.vector.tensor_tensor(res[:, lo:hi], o1[:, lo:hi], o2[:, lo:hi], ADD)
-            nc.sync.dma_start(out=out[:, lo:hi], in_=res[:, lo:hi])
+            queue.dma_start(out=out[:, lo:hi], in_=res[:, lo:hi])
 
-        for n, part in enumerate(OUT_PARTS):
-            pick(o1, pos1_t, gates[:, 0], part)
-            if n > 0:
-                finish(OUT_PARTS[n - 1])
-            pick(o2, pos2_t, gates[:, 1], part)
-        finish(OUT_PARTS[-1])
+        wide, short, last = OUT_PARTS
+        pick(o1, pos1_t, gates[:, 0], wide)
+        pick(o2, pos2_t, gates[:, 1], wide)
+        pick(o1, pos1_t, gates[:, 0], short)
+        finish(wide, nc.sync)
+        pick(o2, pos2_t, gates[:, 1], short)
+        pick(o1, pos1_t, gates[:, 0], last)
+        pick(o2, pos2_t, gates[:, 1], last)
+        finish(short, nc.sync)
+        finish(last, nc.scalar)

@@ -258,18 +258,18 @@ def tile_moe_cap2_glu_gelu_kernel(
             lo, hi = part
             nc.vector.tensor_tensor(o[:, lo:hi], y[:].indirect(pos_t[:, lo // 16 : hi // 16]), gate_t[:, lo:hi], MULT)
 
-        def finish(part, queue):
+        def finish(part):
             lo, hi = part
             nc.vector.tensor_tensor(res[:, lo:hi], o1[:, lo:hi], o2[:, lo:hi], ADD)
-            queue.dma_start(out=out[:, lo:hi], in_=res[:, lo:hi])
+            nc.sync.dma_start(out=out[:, lo:hi], in_=res[:, lo:hi])
 
         wide, short, last = OUT_PARTS
         pick(o1, pos1_t, gates[:, 0], wide)
         pick(o2, pos2_t, gates[:, 1], wide)
         pick(o1, pos1_t, gates[:, 0], short)
-        finish(wide, nc.sync)
+        finish(wide)
         pick(o2, pos2_t, gates[:, 1], short)
         pick(o1, pos1_t, gates[:, 0], last)
         pick(o2, pos2_t, gates[:, 1], last)
-        finish(short, nc.sync)
-        finish(last, nc.scalar)
+        finish(short)
+        finish(last)

@@ -23,11 +23,14 @@ ADD = mybir.AluOpType.add
 
 X_BLOCKS = (((256, 160), (256, 160)), ((128, 96), (128, 64)))
 SCALE_GROUPS = ((0, 4), (4, 8))
-QUANT_GROUPS = ((0, 2), (2, 4), (4, 6), (6, 7), (7, 8))
-KEEP_GROUPS = ((0, 4), (4, 7), (7, 8))
-KEEP_BANKS = ("a3", "a1", "y0")
 GATHER_GROUPS = ((0, 1), (1, 2), (2, 4), (4, 6), (6, 8))
-GATHER_TILES = (0, 1, 2, 3, 2)
+ON_GPSIMD = (0, 1)
+A_BANKS = (0, 1, 0, 1, 2, 3, 0, 1)
+B_BANKS = (4, 5, 6, 7, 4, 5, 6, 7)
+TURN_GROUPS = ((2, 4, 0), (4, 6, 4), (0, 2, 1), (6, 7, 6), (7, 8, 7))
+QUANT_GROUPS = ((2, 4), (4, 6), (0, 2), (6, 8))
+KEEP_GROUPS = ((2, 6, 2), (0, 2, 3), (6, 8, 5))
+WARM_PASSES = 3
 OUT_PARTS = ((0, 512), (512, 640), (640, T))
 
 
@@ -62,6 +65,11 @@ def tile_moe_cap2_glu_gelu_kernel(
         xs = held.tile([P, T], U8, name="xs", align_bytes=64)
         zero(s2[:])
         nc.vector.memset(xs[:].bitcast(I32), 0)
+        blank = held.tile([P, 4 * C], BF16, name="blank", align_bytes=64)
+        blank_q = held.tile([P, C], U32, name="blank_q", align_bytes=64)
+        blank_s = held.tile([P, C], U8, name="blank_s", align_bytes=64)
+        nc.vector.memset(blank[:], 0.0)
+        nc.vector.quantize_mx(out=blank_q[:].bitcast(FP8X4), scales=blank_s[:], in_=blank[:])
         w2t = held.tile([P, E, 2 * N], U8, name="w2t", align_bytes=64)
         words = {}
         for g in range(E // 2):
@@ -134,15 +142,15 @@ def tile_moe_cap2_glu_gelu_kernel(
                 )
                 lo, t0 = lo + width, t0 + width
 
-        gq, gs, a_t, b_t, g_t, h_t, xt_t, hi_t, hq_t, hs_t, y_t = [{} for i in range(11)]
+        gq, gs, a_t, b_t, g_t, h_t, hi_t, hq_t, hs_t, y_t = [{} for i in range(10)]
 
         def group_of(groups, e):
-            return [g for g, (e0, e1) in enumerate(groups) if e0 <= e < e1][0]
+            return [g for g, grp in enumerate(groups) if grp[0] <= e < grp[1]][0]
 
         def gather(g):
             e0, e1 = GATHER_GROUPS[g]
-            gq[g] = held.tile([P, (e1 - e0) * C], U32, name=f"gq{GATHER_TILES[g]}", align_bytes=64)
-            gs[g] = held.tile([P, (e1 - e0) * C], U8, name=f"gs{GATHER_TILES[g]}", align_bytes=64)
+            gq[g] = held.tile([P, (e1 - e0) * C], U32, name=f"gq{g}", align_bytes=64)
+            gs[g] = held.tile([P, (e1 - e0) * C], U8, name=f"gs{g}", align_bytes=64)
             lst = offs_t[:, e0 * C // 16 : e1 * C // 16]
             nc.vector.tensor_copy(gq[g][:], xq[:].indirect(lst))
             nc.vector.tensor_copy(gs[g][:], xs[:].indirect(lst))
@@ -150,7 +158,7 @@ def tile_moe_cap2_glu_gelu_kernel(
         def first(i, e):
             g, s = group_of(GATHER_GROUPS, e), group_of(SCALE_GROUPS, e)
             slots = slice((e - GATHER_GROUPS[g][0]) * C, (e - GATHER_GROUPS[g][0] + 1) * C)
-            acc = psum.tile([P, H], F32, name=(f"a{e % 4}", f"b{e % 3}")[i])
+            acc = psum.tile([P, H], F32, name=f"bank{(A_BANKS, B_BANKS)[i][e]}")
             (a_t, b_t)[i][e] = acc
             nc.tensor.matmul_mx(
                 out=acc[:],
@@ -162,91 +170,101 @@ def tile_moe_cap2_glu_gelu_kernel(
                 stop=True,
             )
 
+        def by_pairs(acc):
+            return acc[:].rearrange("s (p u w) -> s u p w", u=2, w=2)
+
         def gelu(e):
             g_t[e] = held.tile([P, 2, P, 2], F32, name=f"g{e}", align_bytes=64)
-            nc.scalar.activation(g_t[e][:], a_t[e][:].rearrange("s (p u w) -> s u p w", u=2, w=2), GELU)
+            nc.scalar.activation(g_t[e][:], by_pairs(a_t[e]), GELU)
+
+        def spill(e):
+            kept = held.tile([P, 2, P, 2], F32, name=f"kept{e}", align_bytes=64)
+            nc.scalar.copy(kept[:], by_pairs(b_t[e]))
+            b_t[e] = kept
 
         def mul(e):
-            h_t[e] = held.tile([P, 2, P, 2], BF16, name=f"h{e}", align_bytes=64)
-            b = b_t[e][:].rearrange("s (p u w) -> s u p w", u=2, w=2)
-            if e == E - 1:
+            h_t[e] = held.tile([P, 2, P, 2], BF16, name="xq" if e == ON_GPSIMD[0] else f"h{e}", align_bytes=64)
+            if e in ON_GPSIMD:
+                flat = "s u p w -> s (u p w)"
+                nc.gpsimd.tensor_tensor(
+                    h_t[e][:].rearrange(flat), b_t[e][:].rearrange(flat), g_t[e][:].rearrange(flat), MULT
+                )
+            elif e == E - 1:
                 for u in range(2):
-                    nc.vector.tensor_tensor(h_t[e][:, u], b[:, u], g_t[e][:, u], MULT)
+                    nc.vector.tensor_tensor(h_t[e][:, u], by_pairs(b_t[e])[:, u], g_t[e][:, u], MULT)
             else:
-                nc.vector.tensor_tensor(h_t[e][:], b, g_t[e][:], MULT)
+                nc.vector.tensor_tensor(h_t[e][:], by_pairs(b_t[e]), g_t[e][:], MULT)
 
-        def turn_bank(e):
-            if e < 4:
-                return f"a{(e + 2 + e // 2) % 4}"
-            return f"a{e % 4}" if e + 3 < E else f"b{e % 3}"
-
-        def turn(e):
-            xt_t[e] = psum.tile([P, 2, P], F32, name=turn_bank(e))
-            pairs = h_t[e][:].rearrange("s u p w -> s (u p w)").bitcast(F32)
-            for u in range(2):
-                nc.tensor.transpose(xt_t[e][:, u], pairs[:, u * P : (u + 1) * P], ident[:])
-
-        def lay(e):
-            g = group_of(QUANT_GROUPS, e)
-            e0, e1 = QUANT_GROUPS[g]
-            if e == e0:
-                hi_t[g] = held.tile([P, (e1 - e0) * C * 4], BF16, name=f"hi{g}", align_bytes=64)
-            mine = hi_t[g][:, (e - e0) * C * 4 : (e - e0 + 1) * C * 4]
-            nc.scalar.copy(mine.bitcast(F32).rearrange("p (s u) -> p s u", u=2), xt_t[e][:].rearrange("p u s -> p s u"))
+        def turn(e0, e1, bank):
+            xt = psum.tile([P, e1 - e0, 2, P], F32, name=f"bank{bank}")
+            for e in range(e0, e1):
+                pairs = h_t[e][:].rearrange("s u p w -> s (u p w)").bitcast(F32)
+                for u in range(2):
+                    nc.tensor.transpose(xt[:, e - e0, u], pairs[:, u * P : (u + 1) * P], ident[:])
+            g = group_of(QUANT_GROUPS, e0)
+            q0, q1 = QUANT_GROUPS[g][:2]
+            if e0 == q0:
+                hi_t[g] = held.tile([P, (q1 - q0) * C * 4], BF16, name=f"hi{g}", align_bytes=64)
+            mine = hi_t[g][:, (e0 - q0) * C * 4 : (e1 - q0) * C * 4]
+            copy = nc.vector.tensor_copy if e0 == E - 2 else nc.scalar.copy
+            copy(mine.bitcast(F32).rearrange("p (e s u) -> p e s u", s=C, u=2), xt[:].rearrange("p e u s -> p e s u"))
 
         def quant(g):
-            e0, e1 = QUANT_GROUPS[g]
-            hq_t[g] = held.tile([P, (e1 - e0) * C], U32, name=f"g{E - 1}" if g == 1 else f"hq{g}", align_bytes=64)
+            e0, e1 = QUANT_GROUPS[g][:2]
+            hq_t[g] = held.tile([P, (e1 - e0) * C], U32, name=f"g{E - 1}" if g == 0 else f"hq{g}", align_bytes=64)
             hs_t[g] = held.tile([P, (e1 - e0) * C], U8, name=f"hs{g}", align_bytes=64)
             nc.vector.quantize_mx(out=hq_t[g][:].bitcast(FP8X4), scales=hs_t[g][:], in_=hi_t[g][:])
 
-        def second(e):
-            g, k = group_of(QUANT_GROUPS, e), group_of(KEEP_GROUPS, e)
-            k0, k1 = KEEP_GROUPS[k]
-            if e == k0:
-                y_t[k] = psum.tile([P, (k1 - k0) * C], F32, name=KEEP_BANKS[k])
-            cols = slice((e - QUANT_GROUPS[g][0]) * C, (e - QUANT_GROUPS[g][0] + 1) * C)
+        def second(k):
+            e0, e1, bank = KEEP_GROUPS[k]
+            y_t[k] = psum.tile([P, (e1 - e0) * C], F32, name=f"bank{bank}")
+            for e in range(e0, e1):
+                g = group_of(QUANT_GROUPS, e)
+                cols = slice((e - QUANT_GROUPS[g][0]) * C, (e - QUANT_GROUPS[g][0] + 1) * C)
+                nc.tensor.matmul_mx(
+                    out=y_t[k][:, (e - e0) * C : (e - e0 + 1) * C],
+                    lhsT=w2t[:, e].bitcast(FP4X4),
+                    lhsT_scale=s2[:, e],
+                    rhs=hq_t[g][:, cols].bitcast(FP8X4),
+                    rhs_scale=hs_t[g][:, cols],
+                    start=True,
+                    stop=True,
+                )
+
+        def keep(k):
+            e0, e1 = KEEP_GROUPS[k][:2]
+            copy = nc.vector.tensor_copy if k == 1 else nc.scalar.copy
+            copy(y[:, e0 * C : e1 * C], y_t[k][:])
+
+        for n in range(WARM_PASSES):
+            idle = psum.tile([P, H], F32, name="bank7")
             nc.tensor.matmul_mx(
-                out=y_t[k][:, (e - k0) * C : (e - k0 + 1) * C],
-                lhsT=w2t[:, e].bitcast(FP4X4),
-                lhsT_scale=s2[:, e],
-                rhs=hq_t[g][:, cols].bitcast(FP8X4),
-                rhs_scale=hs_t[g][:, cols],
+                out=idle[:],
+                lhsT=blank_q[:].bitcast(FP8X4),
+                lhsT_scale=blank_s[:],
+                rhs=planes[0, 0][:, 0:2].rearrange("p e n -> p (e n)").bitcast(FP4X4),
+                rhs_scale=planes[0, 0][:, 0],
                 start=True,
                 stop=True,
             )
 
-        def keep(k):
-            k0, k1 = KEEP_GROUPS[k]
-            if k == 1:
-                nc.vector.tensor_copy(y[:, k0 * C : k1 * C], y_t[k][:])
-            else:
-                nc.scalar.copy(y[:, k0 * C : k1 * C], y_t[k][:])
-
-        for g in range(4):
+        for g in range(len(GATHER_GROUPS)):
             gather(g)
-        for e in range(4):
-            first(0, e)
-            if e < 3:
+        for e0 in range(0, E, 2):
+            for e in (e0, e0 + 1):
+                first(0, e)
+                gelu(e)
+            for e in (e0, e0 + 1):
                 first(1, e)
-            gelu(e)
-        for e in range(E):
-            mul(e)
-            if e + 3 < E:
-                first(1, e + 3)
-            if e == 0:
-                gather(4)
-            if e + 4 < E:
-                first(0, e + 4)
-                gelu(e + 4)
-            turn(e)
-            lay(e)
-            if e == 1:
-                quant(0)
-        for g in range(1, len(QUANT_GROUPS)):
+                if e in ON_GPSIMD:
+                    spill(e)
+                mul(e)
+        for grp in TURN_GROUPS:
+            turn(*grp)
+        for g in range(len(QUANT_GROUPS)):
             quant(g)
-        for e in range(E):
-            second(e)
+        for k in range(len(KEEP_GROUPS)):
+            second(k)
         for k in range(len(KEEP_GROUPS)):
             keep(k)
 

@@ -21,16 +21,16 @@ GELU = mybir.ActivationFunctionType.Gelu_apprx_tanh
 MULT = mybir.AluOpType.mult
 ADD = mybir.AluOpType.add
 
-X_BLOCKS = (((256, 160), (256, 160)), ((128, 96), (128, 64)))
-SCALE_GROUPS = ((0, 4), (4, 8))
+X_BLOCK = 256
+X_ON_VECTOR = ((256, 256, 0), (256, 192, 0))
+SCALE_GROUPS = (((0, 4), (4, 8)), ((0, 8),))
 GATHER_GROUPS = ((0, 1), (1, 2), (2, 4), (4, 6), (6, 8))
-ON_GPSIMD = (0, 1)
-A_BANKS = (0, 1, 0, 1, 2, 3, 0, 1)
+ON_GPSIMD = (0,)
+A_BANKS = (0, 1, 2, 3, 0, 1, 2, 3)
 B_BANKS = (4, 5, 6, 7, 4, 5, 6, 7)
-TURN_GROUPS = ((2, 4, 0), (4, 6, 4), (0, 2, 1), (6, 7, 6), (7, 8, 7))
-QUANT_GROUPS = ((2, 4), (4, 6), (0, 2), (6, 8))
-KEEP_GROUPS = ((2, 6, 2), (0, 2, 3), (6, 8, 5))
-WARM_PASSES = 3
+TURN_GROUPS = ((0, 2, 1), (2, 4, 2), (4, 6, 0), (6, 7, 6), (7, 8, 7))
+QUANT_GROUPS = ((0, 2), (2, 4), (4, 6), (6, 7), (7, 8))
+KEEP_GROUPS = ((0, 4, 3), (4, 7, 4), (7, 8, 5))
 OUT_PARTS = ((0, 512), (512, 640), (640, T))
 
 
@@ -57,31 +57,24 @@ def tile_moe_cap2_glu_gelu_kernel(
         make_identity(nc, ident[:])
 
         planes = {}
-        for g, (e0, e1) in enumerate(SCALE_GROUPS):
-            for i in range(2):
-                planes[i, g] = held.tile([P, e1 - e0, H], U8, name=f"plane{i}_{g}", align_bytes=64)
-                zero(planes[i, g][:])
+        for i, g in ((0, 0), (1, 0), (0, 1)):
+            e0, e1 = SCALE_GROUPS[i][g]
+            planes[i, g] = held.tile([P, e1 - e0, H], U8, name=f"plane{i}_{g}", align_bytes=64)
+            zero(planes[i, g][:])
         s2 = held.tile([P, E, N], U8, name="s2", align_bytes=64)
         xs = held.tile([P, T], U8, name="xs", align_bytes=64)
         zero(s2[:])
         nc.vector.memset(xs[:].bitcast(I32), 0)
-        blank = held.tile([P, 4 * C], BF16, name="blank", align_bytes=64)
-        blank_q = held.tile([P, C], U32, name="blank_q", align_bytes=64)
-        blank_s = held.tile([P, C], U8, name="blank_s", align_bytes=64)
-        nc.vector.memset(blank[:], 0.0)
-        nc.vector.quantize_mx(out=blank_q[:].bitcast(FP8X4), scales=blank_s[:], in_=blank[:])
         w2t = held.tile([P, E, 2 * N], U8, name="w2t", align_bytes=64)
         words = {}
         for g in range(E // 2):
             for i in range(2):
                 words[i, g] = held.tile([P, 2, 2 * H], U8, name=f"words{i}_{g}", align_bytes=64)
-        widths = [sum(w for w, v in blocks) for blocks in X_BLOCKS]
-        raw = [held.tile([P, 4, w], F32, name=f"raw{c}") for c, w in enumerate(widths)]
+        raw = [held.tile([P, 2, T], F32, name=f"raw{c}") for c in range(2)]
         gates = held.tile([P, 2, T], F32, name="gates")
 
         def load_x(c):
-            t0 = sum(widths[:c])
-            nc.sync.dma_start(out=raw[c][:], in_=xT.rearrange("(p j) w -> p j w", j=4)[:, :, t0 : t0 + widths[c]])
+            nc.sync.dma_start(out=raw[c][:], in_=xT.rearrange("(p j) w -> p j w", j=4)[:, 2 * c : 2 * c + 2])
 
         def load_scales(plane, scales, e0, e1):
             for r in range(4):
@@ -91,7 +84,7 @@ def tile_moe_cap2_glu_gelu_kernel(
                 )
 
         def load_plane(i, g):
-            load_scales(planes[i, g], (w1_scales, w3_scales)[i], *SCALE_GROUPS[g])
+            load_scales(planes[i, g], (w1_scales, w3_scales)[i], *SCALE_GROUPS[i][g])
 
         def load_words(i, g):
             nc.sync.dma_start(
@@ -108,7 +101,6 @@ def tile_moe_cap2_glu_gelu_kernel(
         load_plane(1, 0)
         load_words(0, 1)
         load_words(1, 1)
-        load_plane(1, 1)
         load_plane(0, 1)
         load_words(0, 2)
         load_words(1, 2)
@@ -121,26 +113,20 @@ def tile_moe_cap2_glu_gelu_kernel(
         nc.sync.dma_start(out=gates[:], in_=gate.rearrange("i p t -> p i t"))
 
         xq = held.tile([P, T], U32, name="xq", align_bytes=64)
-        t0 = 0
-        for c, blocks in enumerate(X_BLOCKS):
-            xb = held.tile([P, widths[c], 4], BF16, name=f"xb{c}", align_bytes=64)
-            src = raw[c][:].rearrange("p j (q i) -> p q j i", i=4)
-            dst = xb[:].rearrange("p (q i) j -> p q j i", i=4)
-            lo = 0
-            for width, on_vector in blocks:
-                q0, q1, q2 = lo // 4, (lo + on_vector) // 4, (lo + width) // 4
-                nc.vector.tensor_copy(out=dst[:, q0:q1], in_=src[:, q0:q1])
-                nc.scalar.copy(out=dst[:, q1:q2], in_=src[:, q1:q2])
-                lo = lo + width
-            lo = 0
-            for width, on_vector in blocks:
-                cols = slice(t0, t0 + width)
-                nc.vector.quantize_mx(
-                    out=xq[:, cols].bitcast(FP8X4),
-                    scales=xs[:, cols],
-                    in_=xb[:, lo : lo + width].rearrange("p w j -> p (w j)"),
-                )
-                lo, t0 = lo + width, t0 + width
+        xb = [held.tile([P, X_BLOCK, 4], BF16, name=f"xb{b}", align_bytes=64) for b in range(T // X_BLOCK)]
+        for c, shares in enumerate(X_ON_VECTOR):
+            for b, share in enumerate(shares):
+                src = raw[c][:, :, b * X_BLOCK : (b + 1) * X_BLOCK].rearrange("p j (q i) -> p q j i", i=4)
+                dst = xb[b][:, :, 2 * c : 2 * c + 2].rearrange("p (q i) j -> p q j i", i=4)
+                if share > 0:
+                    nc.vector.tensor_copy(out=dst[:, : share // 4], in_=src[:, : share // 4])
+                if share < X_BLOCK:
+                    nc.scalar.copy(out=dst[:, share // 4 :], in_=src[:, share // 4 :])
+        for b in range(T // X_BLOCK):
+            cols = slice(b * X_BLOCK, (b + 1) * X_BLOCK)
+            nc.vector.quantize_mx(
+                out=xq[:, cols].bitcast(FP8X4), scales=xs[:, cols], in_=xb[b][:].rearrange("p w j -> p (w j)")
+            )
 
         gq, gs, a_t, b_t, g_t, h_t, hi_t, hq_t, hs_t, y_t = [{} for i in range(10)]
 
@@ -156,7 +142,7 @@ def tile_moe_cap2_glu_gelu_kernel(
             nc.vector.tensor_copy(gs[g][:], xs[:].indirect(lst))
 
         def first(i, e):
-            g, s = group_of(GATHER_GROUPS, e), group_of(SCALE_GROUPS, e)
+            g, s = group_of(GATHER_GROUPS, e), group_of(SCALE_GROUPS[i], e)
             slots = slice((e - GATHER_GROUPS[g][0]) * C, (e - GATHER_GROUPS[g][0] + 1) * C)
             acc = psum.tile([P, H], F32, name=f"bank{(A_BANKS, B_BANKS)[i][e]}")
             (a_t, b_t)[i][e] = acc
@@ -165,7 +151,7 @@ def tile_moe_cap2_glu_gelu_kernel(
                 lhsT=gq[g][:, slots].bitcast(FP8X4),
                 lhsT_scale=gs[g][:, slots],
                 rhs=words[i, e // 2][:, e % 2].bitcast(FP4X4),
-                rhs_scale=planes[i, s][:, e - SCALE_GROUPS[s][0]],
+                rhs_scale=planes[i, s][:, e - SCALE_GROUPS[i][s][0]],
                 start=True,
                 stop=True,
             )
@@ -206,12 +192,13 @@ def tile_moe_cap2_glu_gelu_kernel(
             if e0 == q0:
                 hi_t[g] = held.tile([P, (q1 - q0) * C * 4], BF16, name=f"hi{g}", align_bytes=64)
             mine = hi_t[g][:, (e0 - q0) * C * 4 : (e1 - q0) * C * 4]
-            copy = nc.vector.tensor_copy if e0 == E - 2 else nc.scalar.copy
-            copy(mine.bitcast(F32).rearrange("p (e s u) -> p e s u", s=C, u=2), xt[:].rearrange("p e u s -> p e s u"))
+            nc.scalar.copy(
+                mine.bitcast(F32).rearrange("p (e s u) -> p e s u", s=C, u=2), xt[:].rearrange("p e u s -> p e s u")
+            )
 
         def quant(g):
             e0, e1 = QUANT_GROUPS[g][:2]
-            hq_t[g] = held.tile([P, (e1 - e0) * C], U32, name=f"g{E - 1}" if g == 0 else f"hq{g}", align_bytes=64)
+            hq_t[g] = held.tile([P, (e1 - e0) * C], U32, name=f"hq{g}", align_bytes=64)
             hs_t[g] = held.tile([P, (e1 - e0) * C], U8, name=f"hs{g}", align_bytes=64)
             nc.vector.quantize_mx(out=hq_t[g][:].bitcast(FP8X4), scales=hs_t[g][:], in_=hi_t[g][:])
 
@@ -236,30 +223,20 @@ def tile_moe_cap2_glu_gelu_kernel(
             copy = nc.vector.tensor_copy if k == 1 else nc.scalar.copy
             copy(y[:, e0 * C : e1 * C], y_t[k][:])
 
-        for n in range(WARM_PASSES):
-            idle = psum.tile([P, H], F32, name="bank7")
-            nc.tensor.matmul_mx(
-                out=idle[:],
-                lhsT=blank_q[:].bitcast(FP8X4),
-                lhsT_scale=blank_s[:],
-                rhs=planes[0, 0][:, 0:2].rearrange("p e n -> p (e n)").bitcast(FP4X4),
-                rhs_scale=planes[0, 0][:, 0],
-                start=True,
-                stop=True,
-            )
-
         for g in range(len(GATHER_GROUPS)):
             gather(g)
-        for e0 in range(0, E, 2):
-            for e in (e0, e0 + 1):
+        for e0, e1 in ((0, 2), (2, 4), (4, 6), (6, 8)):
+            for e in range(e0, e1):
                 first(0, e)
                 gelu(e)
-            for e in (e0, e0 + 1):
+            if e1 == E:
+                turn(*TURN_GROUPS[0])
+            for e in range(e0, e1):
                 first(1, e)
                 if e in ON_GPSIMD:
                     spill(e)
                 mul(e)
-        for grp in TURN_GROUPS:
+        for grp in TURN_GROUPS[1:]:
             turn(*grp)
         for g in range(len(QUANT_GROUPS)):
             quant(g)

@@ -20,9 +20,9 @@ FP4X4 = mybir.dt.float4_e2m1fn_x4
 GELU = mybir.ActivationFunctionType.Gelu_apprx_tanh
 MULT = mybir.AluOpType.mult
 ADD = mybir.AluOpType.add
+COPY = mybir.ActivationFunctionType.Copy
 
-X_BLOCK = 256
-X_ON_VECTOR = ((256, 256, 0), (256, 192, 0))
+X_BLOCKS = (((256, 160), (256, 160)), ((128, 96), (128, 64)))
 SCALE_GROUPS = (((0, 4), (4, 8)), ((0, 8),))
 GATHER_GROUPS = ((0, 1), (1, 2), (2, 4), (4, 6), (6, 8))
 ON_GPSIMD = (0,)
@@ -31,7 +31,10 @@ B_BANKS = (4, 5, 6, 7, 4, 5, 6, 7)
 TURN_GROUPS = ((0, 2, 1), (2, 4, 2), (4, 6, 0), (6, 7, 6), (7, 8, 7))
 QUANT_GROUPS = ((0, 2), (2, 4), (4, 6), (6, 7), (7, 8))
 KEEP_GROUPS = ((0, 4, 3), (4, 7, 4), (7, 8, 5))
-OUT_PARTS = ((0, 512), (512, 640), (640, T))
+TURNED = 256
+FORTH_BANKS = ((0, 1, 2), (6, 7, 3))
+SUM_BANKS = (4, 5, 2)
+FUSED_PARTS = ((TURNED, 512), (512, 640), (640, T))
 
 
 def tile_moe_cap2_glu_gelu_kernel(
@@ -70,11 +73,14 @@ def tile_moe_cap2_glu_gelu_kernel(
         for g in range(E // 2):
             for i in range(2):
                 words[i, g] = held.tile([P, 2, 2 * H], U8, name=f"words{i}_{g}", align_bytes=64)
-        raw = [held.tile([P, 2, T], F32, name=f"raw{c}") for c in range(2)]
-        gates = held.tile([P, 2, T], F32, name="gates")
+        widths = [sum(w for w, v in blocks) for blocks in X_BLOCKS]
+        raw = [held.tile([P, 4, w], F32, name=f"raw{c}") for c, w in enumerate(widths)]
+        gates = held.tile([P, 2, T - TURNED], F32, name="gates")
+        gate_cols = [held.tile([P, TURNED // P], F32, name=f"gate_cols{i}") for i in range(2)]
 
         def load_x(c):
-            nc.sync.dma_start(out=raw[c][:], in_=xT.rearrange("(p j) w -> p j w", j=4)[:, 2 * c : 2 * c + 2])
+            t0 = sum(widths[:c])
+            nc.sync.dma_start(out=raw[c][:], in_=xT.rearrange("(p j) w -> p j w", j=4)[:, :, t0 : t0 + widths[c]])
 
         def load_scales(plane, scales, e0, e1):
             for r in range(4):
@@ -110,23 +116,32 @@ def tile_moe_cap2_glu_gelu_kernel(
         load_scales(s2, w2_scales, 0, E)
         nc.sync.dma_start(pos1_t[:], pos1)
         nc.sync.dma_start(pos2_t[:], pos2)
-        nc.sync.dma_start(out=gates[:], in_=gate.rearrange("i p t -> p i t"))
+        with nc.allow_non_contiguous_dma(reason="one gate value a token and partition"):
+            for i in range(2):
+                nc.sync.dma_start(out=gate_cols[i][:], in_=gate[i, 0, :TURNED].rearrange("(c p) -> p c", p=P))
+        nc.sync.dma_start(out=gates[:], in_=gate.rearrange("i p t -> p i t")[:, :, TURNED:])
 
         xq = held.tile([P, T], U32, name="xq", align_bytes=64)
-        xb = [held.tile([P, X_BLOCK, 4], BF16, name=f"xb{b}", align_bytes=64) for b in range(T // X_BLOCK)]
-        for c, shares in enumerate(X_ON_VECTOR):
-            for b, share in enumerate(shares):
-                src = raw[c][:, :, b * X_BLOCK : (b + 1) * X_BLOCK].rearrange("p j (q i) -> p q j i", i=4)
-                dst = xb[b][:, :, 2 * c : 2 * c + 2].rearrange("p (q i) j -> p q j i", i=4)
-                if share > 0:
-                    nc.vector.tensor_copy(out=dst[:, : share // 4], in_=src[:, : share // 4])
-                if share < X_BLOCK:
-                    nc.scalar.copy(out=dst[:, share // 4 :], in_=src[:, share // 4 :])
-        for b in range(T // X_BLOCK):
-            cols = slice(b * X_BLOCK, (b + 1) * X_BLOCK)
-            nc.vector.quantize_mx(
-                out=xq[:, cols].bitcast(FP8X4), scales=xs[:, cols], in_=xb[b][:].rearrange("p w j -> p (w j)")
-            )
+        t0 = 0
+        for c, blocks in enumerate(X_BLOCKS):
+            xb = held.tile([P, widths[c], 4], BF16, name=f"xb{c}", align_bytes=64)
+            src = raw[c][:].rearrange("p j (q i) -> p q j i", i=4)
+            dst = xb[:].rearrange("p (q i) j -> p q j i", i=4)
+            lo = 0
+            for width, on_vector in blocks:
+                q0, q1, q2 = lo // 4, (lo + on_vector) // 4, (lo + width) // 4
+                nc.vector.tensor_copy(out=dst[:, q0:q1], in_=src[:, q0:q1])
+                nc.scalar.copy(out=dst[:, q1:q2], in_=src[:, q1:q2])
+                lo = lo + width
+            lo = 0
+            for width, on_vector in blocks:
+                cols = slice(t0, t0 + width)
+                nc.vector.quantize_mx(
+                    out=xq[:, cols].bitcast(FP8X4),
+                    scales=xs[:, cols],
+                    in_=xb[:, lo : lo + width].rearrange("p w j -> p (w j)"),
+                )
+                lo, t0 = lo + width, t0 + width
 
         gq, gs, a_t, b_t, g_t, h_t, hi_t, hq_t, hs_t, y_t = [{} for i in range(10)]
 
@@ -245,26 +260,58 @@ def tile_moe_cap2_glu_gelu_kernel(
         for k in range(len(KEEP_GROUPS)):
             keep(k)
 
-        o1 = held.tile([P, T], F32, name="o1")
-        o2 = held.tile([P, T], F32, name="o2")
-        res = held.tile([P, T], F32, name="res")
+        lists = (pos1_t, pos2_t)
+        blocks = range(TURNED // P)
+        picked, scaled, sums = {}, {}, {}
 
-        def pick(o, pos_t, gate_t, part):
+        def fetch(i):
+            picked[i] = held.tile([P, TURNED], F32, name=f"picked{i}")
+            nc.vector.tensor_copy(picked[i][:], y[:].indirect(lists[i][:, : TURNED // 16]))
+
+        def weigh(i, c):
+            turned = psum.tile([P, P], F32, name=f"bank{FORTH_BANKS[i][c]}")
+            nc.tensor.transpose(turned[:], picked[i][:, c * P : (c + 1) * P], ident[:])
+            scaled[i, c] = held.tile([P, P], F32, name=f"scaled{i}_{c}")
+            nc.scalar.activation(scaled[i, c][:], turned[:], COPY, scale=gate_cols[i][:, c : c + 1])
+
+        def back(i, c):
+            if i == 0:
+                sums[c] = psum.tile([P, P], F32, name=f"bank{SUM_BANKS[c]}")
+            nc.tensor.matmul(sums[c][:], lhsT=scaled[i, c][:], rhs=ident[:], start=i == 0, stop=i == 1, is_transpose=True)
+
+        weighted = {}
+
+        def pick(i, part, name):
             lo, hi = part
-            nc.vector.tensor_tensor(o[:, lo:hi], y[:].indirect(pos_t[:, lo // 16 : hi // 16]), gate_t[:, lo:hi], MULT)
+            weighted[i, lo] = held.tile([P, hi - lo], F32, name=name)
+            nc.vector.tensor_tensor(
+                weighted[i, lo][:], y[:].indirect(lists[i][:, lo // 16 : hi // 16]), gates[:, i, lo - TURNED : hi - TURNED], MULT
+            )
 
-        def finish(part):
+        def finish(part, skip):
             lo, hi = part
-            nc.vector.tensor_tensor(res[:, lo:hi], o1[:, lo:hi], o2[:, lo:hi], ADD)
-            nc.sync.dma_start(out=out[:, lo:hi], in_=res[:, lo:hi])
+            total = held.tile([P, hi - lo], F32, name=f"total{lo}")
+            nc.vector.tensor_tensor(total[:], weighted[0, lo - skip][:, skip : skip + hi - lo], weighted[1, lo][:], ADD)
+            nc.sync.dma_start(out=out[:, lo:hi], in_=total[:])
 
-        wide, short, last = OUT_PARTS
-        pick(o1, pos1_t, gates[:, 0], wide)
-        pick(o2, pos2_t, gates[:, 1], wide)
-        pick(o1, pos1_t, gates[:, 0], short)
-        finish(wide)
-        pick(o2, pos2_t, gates[:, 1], short)
-        pick(o1, pos1_t, gates[:, 0], last)
-        pick(o2, pos2_t, gates[:, 1], last)
-        finish(short)
-        finish(last)
+        for i in range(2):
+            fetch(i)
+        for i in range(2):
+            for c in blocks:
+                weigh(i, c)
+        for i in range(2):
+            for c in blocks:
+                back(i, c)
+        res = held.tile([P, TURNED], F32, name="res")
+        for c in blocks:
+            nc.scalar.copy(res[:, c * P : (c + 1) * P], sums[c][:])
+        nc.sync.dma_start(out=out[:, :TURNED], in_=res[:])
+        wide, short, last = FUSED_PARTS
+        pick(0, wide, "first0")
+        pick(1, wide, "second0")
+        pick(0, (short[0], last[1]), "first1")
+        finish(wide, 0)
+        pick(1, short, "scaled1_0")
+        pick(1, last, "scaled1_1")
+        finish(short, short[0] - short[0])
+        finish(last, last[0] - short[0])

@@ -22,7 +22,7 @@ MULT = mybir.AluOpType.mult
 ADD = mybir.AluOpType.add
 COPY = mybir.ActivationFunctionType.Copy
 
-X_BLOCKS = (((256, 160), (256, 160)), ((128, 96), (128, 64)))
+X_BLOCKS = (((256, 160), (128, 80)), ((256, 144),), ((128, 72),))
 SCALE_GROUPS = (((0, 4), (4, 8)), ((0, 8),))
 GATHER_GROUPS = ((0, 1), (1, 2), (2, 4), (4, 6), (6, 8))
 ON_GPSIMD = (0,)
@@ -31,6 +31,7 @@ B_BANKS = (4, 5, 6, 7, 4, 5, 6, 7)
 TURN_GROUPS = ((0, 2, 1), (2, 4, 2), (4, 6, 0), (6, 7, 6), (7, 8, 7))
 QUANT_GROUPS = ((0, 2), (2, 4), (4, 6), (6, 7), (7, 8))
 KEEP_GROUPS = ((0, 4, 3), (4, 7, 4), (7, 8, 5))
+WARM_PASSES = 2
 TURNED = 256
 FORTH_BANKS = ((0, 1, 2), (6, 7, 3))
 SUM_BANKS = (4, 5, 2)
@@ -68,6 +69,11 @@ def tile_moe_cap2_glu_gelu_kernel(
         xs = held.tile([P, T], U8, name="xs", align_bytes=64)
         zero(s2[:])
         nc.vector.memset(xs[:].bitcast(I32), 0)
+        blank = held.tile([P, 4 * C], BF16, name="blank", align_bytes=64)
+        blank_q = held.tile([P, C], U32, name="blank_q", align_bytes=64)
+        blank_s = held.tile([P, C], U8, name="blank_s", align_bytes=64)
+        nc.vector.memset(blank[:], 0.0)
+        nc.vector.quantize_mx(out=blank_q[:].bitcast(FP8X4), scales=blank_s[:], in_=blank[:])
         w2t = held.tile([P, E, 2 * N], U8, name="w2t", align_bytes=64)
         words = {}
         for g in range(E // 2):
@@ -76,7 +82,8 @@ def tile_moe_cap2_glu_gelu_kernel(
         widths = [sum(w for w, v in blocks) for blocks in X_BLOCKS]
         raw = [held.tile([P, 4, w], F32, name=f"raw{c}") for c, w in enumerate(widths)]
         gates = held.tile([P, 2, T - TURNED], F32, name="gates")
-        gate_cols = [held.tile([P, TURNED // P], F32, name=f"gate_cols{i}") for i in range(2)]
+        gate_rows = held.tile([P, P], F32, name="gate_rows")
+        nc.gpsimd.memset(gate_rows[:], 0.0)
 
         def load_x(c):
             t0 = sum(widths[:c])
@@ -100,6 +107,7 @@ def tile_moe_cap2_glu_gelu_kernel(
 
         load_x(0)
         load_x(1)
+        load_x(2)
         nc.sync.dma_start(offs_t[:], offs)
         load_plane(0, 0)
         load_words(0, 0)
@@ -114,11 +122,11 @@ def tile_moe_cap2_glu_gelu_kernel(
         load_words(1, 3)
         nc.sync.dma_start(out=w2t[:].bitcast(I32), in_=w2_words.bitcast(I32).rearrange("e s p n -> p (e s) n"))
         load_scales(s2, w2_scales, 0, E)
+        for i in range(2):
+            rows = slice(i * TURNED // P, (i + 1) * TURNED // P)
+            nc.sync.dma_start(out=gate_rows[rows], in_=gate[i, 0, :TURNED].rearrange("(c p) -> c p", p=P))
         nc.sync.dma_start(pos1_t[:], pos1)
         nc.sync.dma_start(pos2_t[:], pos2)
-        with nc.allow_non_contiguous_dma(reason="one gate value a token and partition"):
-            for i in range(2):
-                nc.sync.dma_start(out=gate_cols[i][:], in_=gate[i, 0, :TURNED].rearrange("(c p) -> p c", p=P))
         nc.sync.dma_start(out=gates[:], in_=gate.rearrange("i p t -> p i t")[:, :, TURNED:])
 
         xq = held.tile([P, T], U32, name="xq", align_bytes=64)
@@ -238,6 +246,18 @@ def tile_moe_cap2_glu_gelu_kernel(
             copy = nc.vector.tensor_copy if k == 1 else nc.scalar.copy
             copy(y[:, e0 * C : e1 * C], y_t[k][:])
 
+        for n in range(WARM_PASSES):
+            idle = psum.tile([P, H], F32, name="bank7")
+            nc.tensor.matmul_mx(
+                out=idle[:],
+                lhsT=blank_q[:].bitcast(FP8X4),
+                lhsT_scale=blank_s[:],
+                rhs=planes[0, 0][:, 0:2].rearrange("p e n -> p (e n)").bitcast(FP4X4),
+                rhs_scale=planes[0, 0][:, 0],
+                start=True,
+                stop=True,
+            )
+
         for g in range(len(GATHER_GROUPS)):
             gather(g)
         for e0, e1 in ((0, 2), (2, 4), (4, 6), (6, 8)):
@@ -260,6 +280,11 @@ def tile_moe_cap2_glu_gelu_kernel(
         for k in range(len(KEEP_GROUPS)):
             keep(k)
 
+        gate_turned = psum.tile([P, P], F32, name="bank1")
+        nc.tensor.transpose(gate_turned[:], gate_rows[:], ident[:])
+        gate_cols = held.tile([P, 2, TURNED // P], F32, name="gate_cols")
+        nc.scalar.copy(gate_cols[:].rearrange("p i c -> p (i c)"), gate_turned[:, : 2 * TURNED // P])
+
         lists = (pos1_t, pos2_t)
         blocks = range(TURNED // P)
         picked, scaled, sums = {}, {}, {}
@@ -272,7 +297,7 @@ def tile_moe_cap2_glu_gelu_kernel(
             turned = psum.tile([P, P], F32, name=f"bank{FORTH_BANKS[i][c]}")
             nc.tensor.transpose(turned[:], picked[i][:, c * P : (c + 1) * P], ident[:])
             scaled[i, c] = held.tile([P, P], F32, name=f"scaled{i}_{c}")
-            nc.scalar.activation(scaled[i, c][:], turned[:], COPY, scale=gate_cols[i][:, c : c + 1])
+            nc.scalar.activation(scaled[i, c][:], turned[:], COPY, scale=gate_cols[:, i, c : c + 1])
 
         def back(i, c):
             if i == 0:
@@ -288,10 +313,10 @@ def tile_moe_cap2_glu_gelu_kernel(
                 weighted[i, lo][:], y[:].indirect(lists[i][:, lo // 16 : hi // 16]), gates[:, i, lo - TURNED : hi - TURNED], MULT
             )
 
-        def finish(part, skip):
+        def finish(part, name):
             lo, hi = part
-            total = held.tile([P, hi - lo], F32, name=f"total{lo}")
-            nc.vector.tensor_tensor(total[:], weighted[0, lo - skip][:, skip : skip + hi - lo], weighted[1, lo][:], ADD)
+            total = held.tile([P, hi - lo], F32, name=name)
+            nc.vector.tensor_tensor(total[:], weighted[0, TURNED][:, lo - TURNED : hi - TURNED], weighted[1, lo][:], ADD)
             nc.sync.dma_start(out=out[:, lo:hi], in_=total[:])
 
         for i in range(2):
@@ -307,11 +332,10 @@ def tile_moe_cap2_glu_gelu_kernel(
             nc.scalar.copy(res[:, c * P : (c + 1) * P], sums[c][:])
         nc.sync.dma_start(out=out[:, :TURNED], in_=res[:])
         wide, short, last = FUSED_PARTS
-        pick(0, wide, "first0")
-        pick(1, wide, "second0")
-        pick(0, (short[0], last[1]), "first1")
-        finish(wide, 0)
-        pick(1, short, "scaled1_0")
-        pick(1, last, "scaled1_1")
-        finish(short, short[0] - short[0])
-        finish(last, last[0] - short[0])
+        pick(0, (TURNED, T), "first")
+        pick(1, wide, "second")
+        pick(1, short, "second_short")
+        finish(wide, "total_wide")
+        pick(1, last, "second_last")
+        finish(short, "scaled1_1")
+        finish(last, "total_last")

@@ -22,7 +22,9 @@ MULT = mybir.AluOpType.mult
 ADD = mybir.AluOpType.add
 COPY = mybir.ActivationFunctionType.Copy
 
-X_BLOCKS = (((256, 160), (128, 80)), ((256, 144),), ((128, 72),))
+X_BLOCK = 256
+X_LOADS = ((0, 0, T), (1, 0, 512), (1, 512, T))
+X_ON_VECTOR = ((256, 256, 0), (256, 48, 128))
 SCALE_GROUPS = (((0, 4), (4, 8)), ((0, 8),))
 GATHER_GROUPS = ((0, 1), (1, 2), (2, 4), (4, 6), (6, 8))
 ON_GPSIMD = (0,)
@@ -31,7 +33,6 @@ B_BANKS = (4, 5, 6, 7, 4, 5, 6, 7)
 TURN_GROUPS = ((0, 2, 1), (2, 4, 2), (4, 6, 0), (6, 7, 6), (7, 8, 7))
 QUANT_GROUPS = ((0, 2), (2, 4), (4, 6), (6, 7), (7, 8))
 KEEP_GROUPS = ((0, 4, 3), (4, 7, 4), (7, 8, 5))
-WARM_PASSES = 2
 TURNED = 256
 FORTH_BANKS = ((0, 1, 2), (6, 7, 3))
 SUM_BANKS = (4, 5, 2)
@@ -69,25 +70,20 @@ def tile_moe_cap2_glu_gelu_kernel(
         xs = held.tile([P, T], U8, name="xs", align_bytes=64)
         zero(s2[:])
         nc.vector.memset(xs[:].bitcast(I32), 0)
-        blank = held.tile([P, 4 * C], BF16, name="blank", align_bytes=64)
-        blank_q = held.tile([P, C], U32, name="blank_q", align_bytes=64)
-        blank_s = held.tile([P, C], U8, name="blank_s", align_bytes=64)
-        nc.vector.memset(blank[:], 0.0)
-        nc.vector.quantize_mx(out=blank_q[:].bitcast(FP8X4), scales=blank_s[:], in_=blank[:])
         w2t = held.tile([P, E, 2 * N], U8, name="w2t", align_bytes=64)
         words = {}
         for g in range(E // 2):
             for i in range(2):
                 words[i, g] = held.tile([P, 2, 2 * H], U8, name=f"words{i}_{g}", align_bytes=64)
-        widths = [sum(w for w, v in blocks) for blocks in X_BLOCKS]
-        raw = [held.tile([P, 4, w], F32, name=f"raw{c}") for c, w in enumerate(widths)]
+        raw = [held.tile([P, 2, t1 - t0], F32, name=f"raw{c}") for c, (half, t0, t1) in enumerate(X_LOADS)]
         gates = held.tile([P, 2, T - TURNED], F32, name="gates")
         gate_rows = held.tile([P, P], F32, name="gate_rows")
         nc.gpsimd.memset(gate_rows[:], 0.0)
 
         def load_x(c):
-            t0 = sum(widths[:c])
-            nc.sync.dma_start(out=raw[c][:], in_=xT.rearrange("(p j) w -> p j w", j=4)[:, :, t0 : t0 + widths[c]])
+            half, t0, t1 = X_LOADS[c]
+            rows = xT.rearrange("(p j) w -> p j w", j=4)
+            nc.sync.dma_start(out=raw[c][:], in_=rows[:, 2 * half : 2 * half + 2, t0:t1])
 
         def load_scales(plane, scales, e0, e1):
             for r in range(4):
@@ -130,26 +126,21 @@ def tile_moe_cap2_glu_gelu_kernel(
         nc.sync.dma_start(out=gates[:], in_=gate.rearrange("i p t -> p i t")[:, :, TURNED:])
 
         xq = held.tile([P, T], U32, name="xq", align_bytes=64)
-        t0 = 0
-        for c, blocks in enumerate(X_BLOCKS):
-            xb = held.tile([P, widths[c], 4], BF16, name=f"xb{c}", align_bytes=64)
-            src = raw[c][:].rearrange("p j (q i) -> p q j i", i=4)
-            dst = xb[:].rearrange("p (q i) j -> p q j i", i=4)
-            lo = 0
-            for width, on_vector in blocks:
-                q0, q1, q2 = lo // 4, (lo + on_vector) // 4, (lo + width) // 4
-                nc.vector.tensor_copy(out=dst[:, q0:q1], in_=src[:, q0:q1])
-                nc.scalar.copy(out=dst[:, q1:q2], in_=src[:, q1:q2])
-                lo = lo + width
-            lo = 0
-            for width, on_vector in blocks:
-                cols = slice(t0, t0 + width)
-                nc.vector.quantize_mx(
-                    out=xq[:, cols].bitcast(FP8X4),
-                    scales=xs[:, cols],
-                    in_=xb[:, lo : lo + width].rearrange("p w j -> p (w j)"),
-                )
-                lo, t0 = lo + width, t0 + width
+        xb = [held.tile([P, X_BLOCK, 4], BF16, name=f"xb{b}", align_bytes=64) for b in range(T // X_BLOCK)]
+        for c, (half, t0, t1) in enumerate(X_LOADS):
+            for b in range(t0 // X_BLOCK, t1 // X_BLOCK):
+                lo, share = b * X_BLOCK - t0, X_ON_VECTOR[half][b]
+                src = raw[c][:, :, lo : lo + X_BLOCK].rearrange("p j (q i) -> p q j i", i=4)
+                dst = xb[b][:, :, 2 * half : 2 * half + 2].rearrange("p (q i) j -> p q j i", i=4)
+                if share > 0:
+                    nc.vector.tensor_copy(out=dst[:, : share // 4], in_=src[:, : share // 4])
+                if share < X_BLOCK:
+                    nc.scalar.copy(out=dst[:, share // 4 :], in_=src[:, share // 4 :])
+        for b in range(T // X_BLOCK):
+            cols = slice(b * X_BLOCK, (b + 1) * X_BLOCK)
+            nc.vector.quantize_mx(
+                out=xq[:, cols].bitcast(FP8X4), scales=xs[:, cols], in_=xb[b][:].rearrange("p w j -> p (w j)")
+            )
 
         gq, gs, a_t, b_t, g_t, h_t, hi_t, hq_t, hs_t, y_t = [{} for i in range(10)]
 
@@ -245,18 +236,6 @@ def tile_moe_cap2_glu_gelu_kernel(
             e0, e1 = KEEP_GROUPS[k][:2]
             copy = nc.vector.tensor_copy if k == 1 else nc.scalar.copy
             copy(y[:, e0 * C : e1 * C], y_t[k][:])
-
-        for n in range(WARM_PASSES):
-            idle = psum.tile([P, H], F32, name="bank7")
-            nc.tensor.matmul_mx(
-                out=idle[:],
-                lhsT=blank_q[:].bitcast(FP8X4),
-                lhsT_scale=blank_s[:],
-                rhs=planes[0, 0][:, 0:2].rearrange("p e n -> p (e n)").bitcast(FP4X4),
-                rhs_scale=planes[0, 0][:, 0],
-                start=True,
-                stop=True,
-            )
 
         for g in range(len(GATHER_GROUPS)):
             gather(g)

@@ -22,17 +22,21 @@ MULT = mybir.AluOpType.mult
 ADD = mybir.AluOpType.add
 COPY = mybir.ActivationFunctionType.Copy
 
-X_BLOCK = 256
 X_LOADS = ((0, 0, T), (1, 0, 512), (1, 512, T))
+X_BLOCKS = ((0, 256), (256, 512), (512, T))
 X_ON_VECTOR = ((256, 256, 0), (256, 48, 128))
 SCALE_GROUPS = (((0, 4), (4, 8)), ((0, 8),))
+WORD_GROUPS = (((0, 2), (2, 4), (4, 6), (6, 8)), ((0, 2), (2, 4), (4, 6), (6, 8)))
+LOADS = (("s", 0, 0), ("w", 0, 0), ("w", 1, 0), ("s", 1, 0), ("w", 0, 1), ("w", 1, 1), ("s", 0, 1), ("w", 0, 2), ("w", 1, 2), ("w", 0, 3), ("w", 1, 3))
 GATHER_GROUPS = ((0, 1), (1, 2), (2, 4), (4, 6), (6, 8))
-ON_GPSIMD = (0,)
+ON_GPSIMD = (2,)
 A_BANKS = (0, 1, 2, 3, 0, 1, 2, 3)
 B_BANKS = (4, 5, 6, 7, 4, 5, 6, 7)
-TURN_GROUPS = ((0, 2, 1), (2, 4, 2), (4, 6, 0), (6, 7, 6), (7, 8, 7))
+TURN_GROUPS = ((0, 2, 2), (2, 4, 2), (4, 6, 3), (6, 7, 1), (7, 8, 0))
 QUANT_GROUPS = ((0, 2), (2, 4), (4, 6), (6, 7), (7, 8))
-KEEP_GROUPS = ((0, 4, 3), (4, 7, 4), (7, 8, 5))
+KEEP_GROUPS = ((0, 4, 4), (4, 6, 5), (6, 7, 6), (7, 8, 7))
+KEEP_ON_VECTOR = (0, 2)
+TAG = {"h2": "xq", "gs3": "g0", "gq4": "g1", "gs4": "h0", "hq0": "words1_3"}
 TURNED = 256
 FORTH_BANKS = ((0, 1, 2), (6, 7, 3))
 SUM_BANKS = (4, 5, 2)
@@ -62,7 +66,7 @@ def tile_moe_cap2_glu_gelu_kernel(
         make_identity(nc, ident[:])
 
         planes = {}
-        for i, g in ((0, 0), (1, 0), (0, 1)):
+        for i, g in [(i, g) for kind, i, g in LOADS if kind == "s"]:
             e0, e1 = SCALE_GROUPS[i][g]
             planes[i, g] = held.tile([P, e1 - e0, H], U8, name=f"plane{i}_{g}", align_bytes=64)
             zero(planes[i, g][:])
@@ -72,9 +76,9 @@ def tile_moe_cap2_glu_gelu_kernel(
         nc.vector.memset(xs[:].bitcast(I32), 0)
         w2t = held.tile([P, E, 2 * N], U8, name="w2t", align_bytes=64)
         words = {}
-        for g in range(E // 2):
-            for i in range(2):
-                words[i, g] = held.tile([P, 2, 2 * H], U8, name=f"words{i}_{g}", align_bytes=64)
+        for i in range(2):
+            for g, (e0, e1) in enumerate(WORD_GROUPS[i]):
+                words[i, g] = held.tile([P, e1 - e0, 2 * H], U8, name=f"words{i}_{g}", align_bytes=64)
         raw = [held.tile([P, 2, t1 - t0], F32, name=f"raw{c}") for c, (half, t0, t1) in enumerate(X_LOADS)]
         gates = held.tile([P, 2, T - TURNED], F32, name="gates")
         gate_rows = held.tile([P, P], F32, name="gate_rows")
@@ -96,26 +100,17 @@ def tile_moe_cap2_glu_gelu_kernel(
             load_scales(planes[i, g], (w1_scales, w3_scales)[i], *SCALE_GROUPS[i][g])
 
         def load_words(i, g):
+            e0, e1 = WORD_GROUPS[i][g]
             nc.sync.dma_start(
                 out=words[i, g][:].bitcast(I32),
-                in_=(w1_words, w3_words)[i].bitcast(I32)[2 * g : 2 * g + 2].rearrange("e s p n -> p (e s) n"),
+                in_=(w1_words, w3_words)[i].bitcast(I32)[e0:e1].rearrange("e s p n -> p (e s) n"),
             )
 
-        load_x(0)
-        load_x(1)
-        load_x(2)
+        for c in range(len(X_LOADS)):
+            load_x(c)
         nc.sync.dma_start(offs_t[:], offs)
-        load_plane(0, 0)
-        load_words(0, 0)
-        load_words(1, 0)
-        load_plane(1, 0)
-        load_words(0, 1)
-        load_words(1, 1)
-        load_plane(0, 1)
-        load_words(0, 2)
-        load_words(1, 2)
-        load_words(0, 3)
-        load_words(1, 3)
+        for kind, i, g in LOADS:
+            (load_plane if kind == "s" else load_words)(i, g)
         nc.sync.dma_start(out=w2t[:].bitcast(I32), in_=w2_words.bitcast(I32).rearrange("e s p n -> p (e s) n"))
         load_scales(s2, w2_scales, 0, E)
         for i in range(2):
@@ -126,20 +121,21 @@ def tile_moe_cap2_glu_gelu_kernel(
         nc.sync.dma_start(out=gates[:], in_=gate.rearrange("i p t -> p i t")[:, :, TURNED:])
 
         xq = held.tile([P, T], U32, name="xq", align_bytes=64)
-        xb = [held.tile([P, X_BLOCK, 4], BF16, name=f"xb{b}", align_bytes=64) for b in range(T // X_BLOCK)]
+        xb = [held.tile([P, t1 - t0, 4], BF16, name=f"xb{b}", align_bytes=64) for b, (t0, t1) in enumerate(X_BLOCKS)]
         for c, (half, t0, t1) in enumerate(X_LOADS):
-            for b in range(t0 // X_BLOCK, t1 // X_BLOCK):
-                lo, share = b * X_BLOCK - t0, X_ON_VECTOR[half][b]
-                src = raw[c][:, :, lo : lo + X_BLOCK].rearrange("p j (q i) -> p q j i", i=4)
+            for b, (b0, b1) in enumerate(X_BLOCKS):
+                if b0 < t0 or b1 > t1:
+                    continue
+                share = X_ON_VECTOR[half][b]
+                src = raw[c][:, :, b0 - t0 : b1 - t0].rearrange("p j (q i) -> p q j i", i=4)
                 dst = xb[b][:, :, 2 * half : 2 * half + 2].rearrange("p (q i) j -> p q j i", i=4)
                 if share > 0:
                     nc.vector.tensor_copy(out=dst[:, : share // 4], in_=src[:, : share // 4])
-                if share < X_BLOCK:
+                if share < b1 - b0:
                     nc.scalar.copy(out=dst[:, share // 4 :], in_=src[:, share // 4 :])
-        for b in range(T // X_BLOCK):
-            cols = slice(b * X_BLOCK, (b + 1) * X_BLOCK)
+        for b, (b0, b1) in enumerate(X_BLOCKS):
             nc.vector.quantize_mx(
-                out=xq[:, cols].bitcast(FP8X4), scales=xs[:, cols], in_=xb[b][:].rearrange("p w j -> p (w j)")
+                out=xq[:, b0:b1].bitcast(FP8X4), scales=xs[:, b0:b1], in_=xb[b][:].rearrange("p w j -> p (w j)")
             )
 
         gq, gs, a_t, b_t, g_t, h_t, hi_t, hq_t, hs_t, y_t = [{} for i in range(10)]
@@ -149,14 +145,14 @@ def tile_moe_cap2_glu_gelu_kernel(
 
         def gather(g):
             e0, e1 = GATHER_GROUPS[g]
-            gq[g] = held.tile([P, (e1 - e0) * C], U32, name=f"gq{g}", align_bytes=64)
-            gs[g] = held.tile([P, (e1 - e0) * C], U8, name=f"gs{g}", align_bytes=64)
+            gq[g] = held.tile([P, (e1 - e0) * C], U32, name=TAG.get(f"gq{g}", f"gq{g}"), align_bytes=64)
+            gs[g] = held.tile([P, (e1 - e0) * C], U8, name=TAG.get(f"gs{g}", f"gs{g}"), align_bytes=64)
             lst = offs_t[:, e0 * C // 16 : e1 * C // 16]
             nc.vector.tensor_copy(gq[g][:], xq[:].indirect(lst))
             nc.vector.tensor_copy(gs[g][:], xs[:].indirect(lst))
 
         def first(i, e):
-            g, s = group_of(GATHER_GROUPS, e), group_of(SCALE_GROUPS[i], e)
+            g, s, w = group_of(GATHER_GROUPS, e), group_of(SCALE_GROUPS[i], e), group_of(WORD_GROUPS[i], e)
             slots = slice((e - GATHER_GROUPS[g][0]) * C, (e - GATHER_GROUPS[g][0] + 1) * C)
             acc = psum.tile([P, H], F32, name=f"bank{(A_BANKS, B_BANKS)[i][e]}")
             (a_t, b_t)[i][e] = acc
@@ -164,7 +160,7 @@ def tile_moe_cap2_glu_gelu_kernel(
                 out=acc[:],
                 lhsT=gq[g][:, slots].bitcast(FP8X4),
                 lhsT_scale=gs[g][:, slots],
-                rhs=words[i, e // 2][:, e % 2].bitcast(FP4X4),
+                rhs=words[i, w][:, e - WORD_GROUPS[i][w][0]].bitcast(FP4X4),
                 rhs_scale=planes[i, s][:, e - SCALE_GROUPS[i][s][0]],
                 start=True,
                 stop=True,
@@ -183,7 +179,7 @@ def tile_moe_cap2_glu_gelu_kernel(
             b_t[e] = kept
 
         def mul(e):
-            h_t[e] = held.tile([P, 2, P, 2], BF16, name="xq" if e == ON_GPSIMD[0] else f"h{e}", align_bytes=64)
+            h_t[e] = held.tile([P, 2, P, 2], BF16, name=TAG.get(f"h{e}", f"h{e}"), align_bytes=64)
             if e in ON_GPSIMD:
                 flat = "s u p w -> s (u p w)"
                 nc.gpsimd.tensor_tensor(
@@ -204,7 +200,7 @@ def tile_moe_cap2_glu_gelu_kernel(
             g = group_of(QUANT_GROUPS, e0)
             q0, q1 = QUANT_GROUPS[g][:2]
             if e0 == q0:
-                hi_t[g] = held.tile([P, (q1 - q0) * C * 4], BF16, name=f"hi{g}", align_bytes=64)
+                hi_t[g] = held.tile([P, (q1 - q0) * C * 4], BF16, name=TAG.get(f"hi{g}", f"hi{g}"), align_bytes=64)
             mine = hi_t[g][:, (e0 - q0) * C * 4 : (e1 - q0) * C * 4]
             nc.scalar.copy(
                 mine.bitcast(F32).rearrange("p (e s u) -> p e s u", s=C, u=2), xt[:].rearrange("p e u s -> p e s u")
@@ -212,7 +208,7 @@ def tile_moe_cap2_glu_gelu_kernel(
 
         def quant(g):
             e0, e1 = QUANT_GROUPS[g][:2]
-            hq_t[g] = held.tile([P, (e1 - e0) * C], U32, name=f"hq{g}", align_bytes=64)
+            hq_t[g] = held.tile([P, (e1 - e0) * C], U32, name=TAG.get(f"hq{g}", f"hq{g}"), align_bytes=64)
             hs_t[g] = held.tile([P, (e1 - e0) * C], U8, name=f"hs{g}", align_bytes=64)
             nc.vector.quantize_mx(out=hq_t[g][:].bitcast(FP8X4), scales=hs_t[g][:], in_=hi_t[g][:])
 
@@ -234,22 +230,39 @@ def tile_moe_cap2_glu_gelu_kernel(
 
         def keep(k):
             e0, e1 = KEEP_GROUPS[k][:2]
-            copy = nc.vector.tensor_copy if k == 1 else nc.scalar.copy
+            copy = nc.vector.tensor_copy if k in KEEP_ON_VECTOR else nc.scalar.copy
             copy(y[:, e0 * C : e1 * C], y_t[k][:])
 
-        for g in range(len(GATHER_GROUPS)):
+        def gate_of(e):
+            first(0, e)
+            gelu(e)
+
+        def product_of(e):
+            first(1, e)
+            if e in ON_GPSIMD:
+                spill(e)
+            mul(e)
+
+        def pair(e0):
+            for step in (gate_of, product_of):
+                for e in (e0, e0 + 1):
+                    step(e)
+
+        for g in range(3):
             gather(g)
-        for e0, e1 in ((0, 2), (2, 4), (4, 6), (6, 8)):
-            for e in range(e0, e1):
-                first(0, e)
-                gelu(e)
-            if e1 == E:
-                turn(*TURN_GROUPS[0])
-            for e in range(e0, e1):
-                first(1, e)
-                if e in ON_GPSIMD:
-                    spill(e)
-                mul(e)
+        pair(0)
+        gather(3)
+        gate_of(2)
+        gate_of(3)
+        first(1, 2)
+        spill(2)
+        first(1, 3)
+        turn(*TURN_GROUPS[0])
+        gather(4)
+        mul(2)
+        mul(3)
+        for e0 in (4, 6):
+            pair(e0)
         for grp in TURN_GROUPS[1:]:
             turn(*grp)
         for g in range(len(QUANT_GROUPS)):

@@ -37,6 +37,8 @@ QUANT_GROUPS = ((0, 2), (2, 4), (4, 6), (6, 7), (7, 8))
 KEEP_GROUPS = ((0, 4, 4), (4, 6, 5), (6, 7, 6), (7, 8, 7))
 KEEP_ON_VECTOR = (0, 2)
 TAG = {"h2": "xq", "gs3": "g0", "gq4": "g1", "gs4": "h0", "hq0": "words1_3"}
+WARM_GROUP = 4
+WARM_PASSES = 2
 TURNED = 256
 FORTH_BANKS = ((0, 1, 2), (6, 7, 3))
 SUM_BANKS = (4, 5, 2)
@@ -143,6 +145,26 @@ def tile_moe_cap2_glu_gelu_kernel(
         def group_of(groups, e):
             return [g for g, grp in enumerate(groups) if grp[0] <= e < grp[1]][0]
 
+        def coded(g):
+            e0, e1 = QUANT_GROUPS[g][:2]
+            hq_t[g] = held.tile([P, (e1 - e0) * C], U32, name=TAG.get(f"hq{g}", f"hq{g}"), align_bytes=64)
+            hs_t[g] = held.tile([P, (e1 - e0) * C], U8, name=f"hs{g}", align_bytes=64)
+
+        coded(WARM_GROUP)
+        nc.vector.memset(hq_t[WARM_GROUP][:].bitcast(I32), 0)
+        nc.vector.memset(hs_t[WARM_GROUP][:].bitcast(I32), 0)
+        idle = psum.tile([P, H], F32, name="bank7")
+        for k in range(WARM_PASSES):
+            nc.tensor.matmul_mx(
+                out=idle[:],
+                lhsT=hq_t[WARM_GROUP][:].bitcast(FP8X4),
+                lhsT_scale=hs_t[WARM_GROUP][:],
+                rhs=planes[0, 0][:, :2].rearrange("p e n -> p (e n)").bitcast(FP4X4),
+                rhs_scale=planes[0, 0][:, 0],
+                start=True,
+                stop=True,
+            )
+
         def gather(g):
             e0, e1 = GATHER_GROUPS[g]
             gq[g] = held.tile([P, (e1 - e0) * C], U32, name=TAG.get(f"gq{g}", f"gq{g}"), align_bytes=64)
@@ -199,7 +221,7 @@ def tile_moe_cap2_glu_gelu_kernel(
                     nc.tensor.transpose(xt[:, e - e0, u], pairs[:, u * P : (u + 1) * P], ident[:])
             g = group_of(QUANT_GROUPS, e0)
             q0, q1 = QUANT_GROUPS[g][:2]
-            if e0 == q0:
+            if g not in hi_t:
                 hi_t[g] = held.tile([P, (q1 - q0) * C * 4], BF16, name=TAG.get(f"hi{g}", f"hi{g}"), align_bytes=64)
             mine = hi_t[g][:, (e0 - q0) * C * 4 : (e1 - q0) * C * 4]
             nc.scalar.copy(
@@ -207,9 +229,8 @@ def tile_moe_cap2_glu_gelu_kernel(
             )
 
         def quant(g):
-            e0, e1 = QUANT_GROUPS[g][:2]
-            hq_t[g] = held.tile([P, (e1 - e0) * C], U32, name=TAG.get(f"hq{g}", f"hq{g}"), align_bytes=64)
-            hs_t[g] = held.tile([P, (e1 - e0) * C], U8, name=f"hs{g}", align_bytes=64)
+            if g != WARM_GROUP:
+                coded(g)
             nc.vector.quantize_mx(out=hq_t[g][:].bitcast(FP8X4), scales=hs_t[g][:], in_=hi_t[g][:])
 
         def second(k):

@@ -37,12 +37,8 @@ QUANT_GROUPS = ((0, 2), (2, 4), (4, 6), (6, 7), (7, 8))
 KEEP_GROUPS = ((0, 4, 4), (4, 6, 5), (6, 7, 6), (7, 8, 7))
 KEEP_ON_VECTOR = (0, 2)
 TAG = {"h2": "xq", "gs3": "g0", "gq4": "g1", "gs4": "h0", "hq0": "words1_3"}
-WARM_GROUP = 4
-WARM_PASSES = 2
-TURNED = 256
-FORTH_BANKS = ((0, 1, 2), (6, 7, 3))
-SUM_BANKS = (4, 5, 2)
-FUSED_PARTS = ((TURNED, 512), (512, 640), (640, T))
+FUSED = 640
+GATE_LOADS = ((1, 0, FUSED), (0, 0, T), (1, FUSED, T))
 
 
 def tile_moe_cap2_glu_gelu_kernel(
@@ -82,9 +78,6 @@ def tile_moe_cap2_glu_gelu_kernel(
             for g, (e0, e1) in enumerate(WORD_GROUPS[i]):
                 words[i, g] = held.tile([P, e1 - e0, 2 * H], U8, name=f"words{i}_{g}", align_bytes=64)
         raw = [held.tile([P, 2, t1 - t0], F32, name=f"raw{c}") for c, (half, t0, t1) in enumerate(X_LOADS)]
-        gates = held.tile([P, 2, T - TURNED], F32, name="gates")
-        gate_rows = held.tile([P, P], F32, name="gate_rows")
-        nc.gpsimd.memset(gate_rows[:], 0.0)
 
         def load_x(c):
             half, t0, t1 = X_LOADS[c]
@@ -115,12 +108,14 @@ def tile_moe_cap2_glu_gelu_kernel(
             (load_plane if kind == "s" else load_words)(i, g)
         nc.sync.dma_start(out=w2t[:].bitcast(I32), in_=w2_words.bitcast(I32).rearrange("e s p n -> p (e s) n"))
         load_scales(s2, w2_scales, 0, E)
-        for i in range(2):
-            rows = slice(i * TURNED // P, (i + 1) * TURNED // P)
-            nc.sync.dma_start(out=gate_rows[rows], in_=gate[i, 0, :TURNED].rearrange("(c p) -> c p", p=P))
         nc.sync.dma_start(pos1_t[:], pos1)
         nc.sync.dma_start(pos2_t[:], pos2)
-        nc.sync.dma_start(out=gates[:], in_=gate.rearrange("i p t -> p i t")[:, :, TURNED:])
+        gates = {}
+        for i, lo, hi in GATE_LOADS:
+            piece = held.tile([P, hi - lo], F32, name=f"gate{i}_{lo}")
+            nc.sync.dma_start(out=piece[:], in_=gate[i, :, lo:hi])
+            for t in range(lo, hi, P):
+                gates[i, t] = (piece, lo)
 
         xq = held.tile([P, T], U32, name="xq", align_bytes=64)
         xb = [held.tile([P, t1 - t0, 4], BF16, name=f"xb{b}", align_bytes=64) for b, (t0, t1) in enumerate(X_BLOCKS)]
@@ -149,21 +144,6 @@ def tile_moe_cap2_glu_gelu_kernel(
             e0, e1 = QUANT_GROUPS[g][:2]
             hq_t[g] = held.tile([P, (e1 - e0) * C], U32, name=TAG.get(f"hq{g}", f"hq{g}"), align_bytes=64)
             hs_t[g] = held.tile([P, (e1 - e0) * C], U8, name=f"hs{g}", align_bytes=64)
-
-        coded(WARM_GROUP)
-        nc.vector.memset(hq_t[WARM_GROUP][:].bitcast(I32), 0)
-        nc.vector.memset(hs_t[WARM_GROUP][:].bitcast(I32), 0)
-        idle = psum.tile([P, H], F32, name="bank7")
-        for k in range(WARM_PASSES):
-            nc.tensor.matmul_mx(
-                out=idle[:],
-                lhsT=hq_t[WARM_GROUP][:].bitcast(FP8X4),
-                lhsT_scale=hs_t[WARM_GROUP][:],
-                rhs=planes[0, 0][:, :2].rearrange("p e n -> p (e n)").bitcast(FP4X4),
-                rhs_scale=planes[0, 0][:, 0],
-                start=True,
-                stop=True,
-            )
 
         def gather(g):
             e0, e1 = GATHER_GROUPS[g]
@@ -229,8 +209,7 @@ def tile_moe_cap2_glu_gelu_kernel(
             )
 
         def quant(g):
-            if g != WARM_GROUP:
-                coded(g)
+            coded(g)
             nc.vector.quantize_mx(out=hq_t[g][:].bitcast(FP8X4), scales=hs_t[g][:], in_=hi_t[g][:])
 
         def second(k):
@@ -293,62 +272,40 @@ def tile_moe_cap2_glu_gelu_kernel(
         for k in range(len(KEEP_GROUPS)):
             keep(k)
 
-        gate_turned = psum.tile([P, P], F32, name="bank1")
-        nc.tensor.transpose(gate_turned[:], gate_rows[:], ident[:])
-        gate_cols = held.tile([P, 2, TURNED // P], F32, name="gate_cols")
-        nc.scalar.copy(gate_cols[:].rearrange("p i c -> p (i c)"), gate_turned[:, : 2 * TURNED // P])
-
         lists = (pos1_t, pos2_t)
-        blocks = range(TURNED // P)
-        picked, scaled, sums = {}, {}, {}
+        picked = [held.tile([P, T], F32, name="picked0"), held.tile([P, T - FUSED], F32, name="picked1")]
+        weighted = [held.tile([P, T], F32, name=f"weighted{i}") for i in range(2)]
 
-        def fetch(i):
-            picked[i] = held.tile([P, TURNED], F32, name=f"picked{i}")
-            nc.vector.tensor_copy(picked[i][:], y[:].indirect(lists[i][:, : TURNED // 16]))
+        def gate_of_tokens(i, lo, hi):
+            tile, start = gates[i, lo]
+            return tile[:, lo - start : hi - start]
 
-        def weigh(i, c):
-            turned = psum.tile([P, P], F32, name=f"bank{FORTH_BANKS[i][c]}")
-            nc.tensor.transpose(turned[:], picked[i][:, c * P : (c + 1) * P], ident[:])
-            scaled[i, c] = held.tile([P, P], F32, name=f"scaled{i}_{c}")
-            nc.scalar.activation(scaled[i, c][:], turned[:], COPY, scale=gate_cols[:, i, c : c + 1])
+        def results(i, lo, hi):
+            return y[:].indirect(lists[i][:, lo // 16 : hi // 16])
 
-        def back(i, c):
-            if i == 0:
-                sums[c] = psum.tile([P, P], F32, name=f"bank{SUM_BANKS[c]}")
-            nc.tensor.matmul(sums[c][:], lhsT=scaled[i, c][:], rhs=ident[:], start=i == 0, stop=i == 1, is_transpose=True)
+        def fetched(i, lo, hi):
+            return picked[i][:, lo - i * FUSED : hi - i * FUSED]
 
-        weighted = {}
+        def fetch(i, lo, hi):
+            nc.scalar.activation(fetched(i, lo, hi), results(i, lo, hi), COPY)
 
-        def pick(i, part, name):
-            lo, hi = part
-            weighted[i, lo] = held.tile([P, hi - lo], F32, name=name)
-            nc.vector.tensor_tensor(
-                weighted[i, lo][:], y[:].indirect(lists[i][:, lo // 16 : hi // 16]), gates[:, i, lo - TURNED : hi - TURNED], MULT
-            )
+        def weigh(i, lo, hi):
+            nc.vector.tensor_tensor(weighted[i][:, lo:hi], fetched(i, lo, hi), gate_of_tokens(i, lo, hi), MULT)
 
-        def finish(part, name):
-            lo, hi = part
-            total = held.tile([P, hi - lo], F32, name=name)
-            nc.vector.tensor_tensor(total[:], weighted[0, TURNED][:, lo - TURNED : hi - TURNED], weighted[1, lo][:], ADD)
+        def finish(lo, hi):
+            total = held.tile([P, hi - lo], F32, name=f"total{lo}")
+            nc.vector.tensor_tensor(total[:], weighted[0][:, lo:hi], weighted[1][:, lo:hi], ADD)
             nc.sync.dma_start(out=out[:, lo:hi], in_=total[:])
 
-        for i in range(2):
-            fetch(i)
-        for i in range(2):
-            for c in blocks:
-                weigh(i, c)
-        for i in range(2):
-            for c in blocks:
-                back(i, c)
-        res = held.tile([P, TURNED], F32, name="res")
-        for c in blocks:
-            nc.scalar.copy(res[:, c * P : (c + 1) * P], sums[c][:])
-        nc.sync.dma_start(out=out[:, :TURNED], in_=res[:])
-        wide, short, last = FUSED_PARTS
-        pick(0, (TURNED, T), "first")
-        pick(1, wide, "second")
-        pick(1, short, "second_short")
-        finish(wide, "total_wide")
-        pick(1, last, "second_last")
-        finish(short, "scaled1_1")
-        finish(last, "total_last")
+        for lo in (0, 256, 512):
+            fetch(0, lo, lo + 256)
+        fetch(1, FUSED, T)
+        nc.vector.tensor_tensor(weighted[1][:, :FUSED], results(1, 0, FUSED), gate_of_tokens(1, 0, FUSED), MULT)
+        weigh(0, 0, 256)
+        weigh(0, 256, 512)
+        finish(0, 256)
+        finish(256, 512)
+        weigh(0, 512, T)
+        weigh(1, FUSED, T)
+        finish(512, FUSED)
+        finish(FUSED, T)

@@ -66,18 +66,18 @@ def tile_moe_cap2_glu_gelu_kernel(
         planes = {}
         for i, g in [(i, g) for kind, i, g in LOADS if kind == "s"]:
             e0, e1 = SCALE_GROUPS[i][g]
-            planes[i, g] = held.tile([P, e1 - e0, H], U8, name=f"plane{i}_{g}", align_bytes=64)
+            planes[i, g] = held.tile([P, e1 - e0, H], U8, name=f"plane{i}_{g}", align_bytes=256)
             zero(planes[i, g][:])
-        s2 = held.tile([P, E, N], U8, name="s2", align_bytes=64)
-        xs = held.tile([P, T], U8, name="xs", align_bytes=64)
+        s2 = held.tile([P, E, N], U8, name="s2", align_bytes=256)
+        xs = held.tile([P, T], U8, name="xs", align_bytes=256)
         zero(s2[:])
         nc.vector.memset(xs[:].bitcast(I32), 0)
-        w2t = held.tile([P, E, 2 * N], U8, name="w2t", align_bytes=64)
+        w2t = held.tile([P, E, 2 * N], U8, name="w2t", align_bytes=256)
         words = {}
         for i in range(2):
             for g, (e0, e1) in enumerate(WORD_GROUPS[i]):
-                words[i, g] = held.tile([P, e1 - e0, 2 * H], U8, name=f"words{i}_{g}", align_bytes=64)
-        raw = [held.tile([P, 2, t1 - t0], F32, name=f"raw{c}") for c, (half, t0, t1) in enumerate(X_LOADS)]
+                words[i, g] = held.tile([P, e1 - e0, 2 * H], U8, name=f"words{i}_{g}", align_bytes=256)
+        raw = [held.tile([P, 2, t1 - t0], F32, name=f"raw{c}", align_bytes=256) for c, (half, t0, t1) in enumerate(X_LOADS)]
 
         def load_x(c):
             half, t0, t1 = X_LOADS[c]
@@ -112,13 +112,13 @@ def tile_moe_cap2_glu_gelu_kernel(
         nc.sync.dma_start(pos2_t[:], pos2)
         gates = {}
         for i, lo, hi in GATE_LOADS:
-            piece = held.tile([P, hi - lo], F32, name=f"gate{i}_{lo}")
+            piece = held.tile([P, hi - lo], F32, name=f"gate{i}_{lo}", align_bytes=256)
             nc.sync.dma_start(out=piece[:], in_=gate[i, :, lo:hi])
             for t in range(lo, hi, P):
                 gates[i, t] = (piece, lo)
 
-        xq = held.tile([P, T], U32, name="xq", align_bytes=64)
-        xb = [held.tile([P, t1 - t0, 4], BF16, name=f"xb{b}", align_bytes=64) for b, (t0, t1) in enumerate(X_BLOCKS)]
+        xq = held.tile([P, T], U32, name="xq", align_bytes=256)
+        xb = [held.tile([P, t1 - t0, 4], BF16, name=f"xb{b}", align_bytes=256) for b, (t0, t1) in enumerate(X_BLOCKS)]
         for c, (half, t0, t1) in enumerate(X_LOADS):
             for b, (b0, b1) in enumerate(X_BLOCKS):
                 if b0 < t0 or b1 > t1:
@@ -142,13 +142,13 @@ def tile_moe_cap2_glu_gelu_kernel(
 
         def coded(g):
             e0, e1 = QUANT_GROUPS[g][:2]
-            hq_t[g] = held.tile([P, (e1 - e0) * C], U32, name=TAG.get(f"hq{g}", f"hq{g}"), align_bytes=64)
-            hs_t[g] = held.tile([P, (e1 - e0) * C], U8, name=f"hs{g}", align_bytes=64)
+            hq_t[g] = held.tile([P, (e1 - e0) * C], U32, name=TAG.get(f"hq{g}", f"hq{g}"), align_bytes=256)
+            hs_t[g] = held.tile([P, (e1 - e0) * C], U8, name=f"hs{g}", align_bytes=256)
 
         def gather(g):
             e0, e1 = GATHER_GROUPS[g]
-            gq[g] = held.tile([P, (e1 - e0) * C], U32, name=TAG.get(f"gq{g}", f"gq{g}"), align_bytes=64)
-            gs[g] = held.tile([P, (e1 - e0) * C], U8, name=TAG.get(f"gs{g}", f"gs{g}"), align_bytes=64)
+            gq[g] = held.tile([P, (e1 - e0) * C], U32, name=TAG.get(f"gq{g}", f"gq{g}"), align_bytes=256)
+            gs[g] = held.tile([P, (e1 - e0) * C], U8, name=TAG.get(f"gs{g}", f"gs{g}"), align_bytes=256)
             lst = offs_t[:, e0 * C // 16 : e1 * C // 16]
             nc.vector.tensor_copy(gq[g][:], xq[:].indirect(lst))
             nc.vector.tensor_copy(gs[g][:], xs[:].indirect(lst))
@@ -172,16 +172,16 @@ def tile_moe_cap2_glu_gelu_kernel(
             return acc[:].rearrange("s (p u w) -> s u p w", u=2, w=2)
 
         def gelu(e):
-            g_t[e] = held.tile([P, 2, P, 2], F32, name=f"g{e}", align_bytes=64)
+            g_t[e] = held.tile([P, 2, P, 2], F32, name=f"g{e}", align_bytes=256)
             nc.scalar.activation(g_t[e][:], by_pairs(a_t[e]), GELU)
 
         def spill(e):
-            kept = held.tile([P, 2, P, 2], F32, name=f"kept{e}", align_bytes=64)
+            kept = held.tile([P, 2, P, 2], F32, name=f"kept{e}", align_bytes=256)
             nc.scalar.copy(kept[:], by_pairs(b_t[e]))
             b_t[e] = kept
 
         def mul(e):
-            h_t[e] = held.tile([P, 2, P, 2], BF16, name=TAG.get(f"h{e}", f"h{e}"), align_bytes=64)
+            h_t[e] = held.tile([P, 2, P, 2], BF16, name=TAG.get(f"h{e}", f"h{e}"), align_bytes=256)
             if e in ON_GPSIMD:
                 flat = "s u p w -> s (u p w)"
                 nc.gpsimd.tensor_tensor(
@@ -202,7 +202,7 @@ def tile_moe_cap2_glu_gelu_kernel(
             g = group_of(QUANT_GROUPS, e0)
             q0, q1 = QUANT_GROUPS[g][:2]
             if g not in hi_t:
-                hi_t[g] = held.tile([P, (q1 - q0) * C * 4], BF16, name=TAG.get(f"hi{g}", f"hi{g}"), align_bytes=64)
+                hi_t[g] = held.tile([P, (q1 - q0) * C * 4], BF16, name=TAG.get(f"hi{g}", f"hi{g}"), align_bytes=256)
             mine = hi_t[g][:, (e0 - q0) * C * 4 : (e1 - q0) * C * 4]
             nc.scalar.copy(
                 mine.bitcast(F32).rearrange("p (e s u) -> p e s u", s=C, u=2), xt[:].rearrange("p e u s -> p e s u")
@@ -293,7 +293,7 @@ def tile_moe_cap2_glu_gelu_kernel(
             nc.vector.tensor_tensor(weighted[i][:, lo:hi], fetched(i, lo, hi), gate_of_tokens(i, lo, hi), MULT)
 
         def finish(lo, hi):
-            total = held.tile([P, hi - lo], F32, name=f"total{lo}")
+            total = held.tile([P, hi - lo], F32, name=f"total{lo}", align_bytes=256)
             nc.vector.tensor_tensor(total[:], weighted[0][:, lo:hi], weighted[1][:, lo:hi], ADD)
             nc.sync.dma_start(out=out[:, lo:hi], in_=total[:])
 

@@ -22,23 +22,23 @@ MULT = mybir.AluOpType.mult
 ADD = mybir.AluOpType.add
 COPY = mybir.ActivationFunctionType.Copy
 
+ALIGN = 256
 X_LOADS = ((0, 0, T), (1, 0, 512), (1, 512, T))
 X_BLOCKS = ((0, 256), (256, 512), (512, T))
 X_ON_VECTOR = ((256, 256, 0), (256, 48, 128))
+W1, W3 = 0, 1
 SCALE_GROUPS = (((0, 4), (4, 8)), ((0, 8),))
-WORD_GROUPS = (((0, 2), (2, 4), (4, 6), (6, 8)), ((0, 2), (2, 4), (4, 6), (6, 8)))
-LOADS = (("s", 0, 0), ("w", 0, 0), ("w", 1, 0), ("s", 1, 0), ("w", 0, 1), ("w", 1, 1), ("s", 0, 1), ("w", 0, 2), ("w", 1, 2), ("w", 0, 3), ("w", 1, 3))
+PAIRS = ((0, 2), (2, 4), (4, 6), (6, 8))
+LOADS = (("s", W1, 0), ("w", W1, 0), ("w", W3, 0), ("s", W3, 0), ("w", W1, 1), ("w", W3, 1), ("s", W1, 1), ("w", W1, 2), ("w", W3, 2), ("w", W1, 3), ("w", W3, 3))
 GATHER_GROUPS = ((0, 1), (1, 2), (2, 4), (4, 6), (6, 8))
 ON_GPSIMD = (2,)
-A_BANKS = (0, 1, 2, 3, 0, 1, 2, 3)
-B_BANKS = (4, 5, 6, 7, 4, 5, 6, 7)
-TURN_GROUPS = ((0, 2, 2), (2, 4, 2), (4, 6, 3), (6, 7, 1), (7, 8, 0))
-QUANT_GROUPS = ((0, 2), (2, 4), (4, 6), (6, 7), (7, 8))
-KEEP_GROUPS = ((0, 4, 4), (4, 6, 5), (6, 7, 6), (7, 8, 7))
+BANKS = ((0, 1, 2, 3, 0, 1, 2, 3), (4, 5, 6, 7, 4, 5, 6, 7))
+TURNS = (((0, 1), 2), ((3, 4), 2), ((5, 2), 3), ((6,), 1), ((7,), 0))
+QUANT_GROUPS = ((0, 1), (3, 4), (5, 2), (6,), (7,))
+KEEP_GROUPS = (((0, 1, 3, 4), 4), ((2, 5), 5), ((6,), 6), ((7,), 7))
 KEEP_ON_VECTOR = (0, 2)
-TAG = {"h2": "xq", "gs3": "g0", "gq4": "g1", "gs4": "h0", "hq0": "words1_3"}
+TAG = {"h2": "xq", "gs3": "g0", "gq4": "g1", "gs4": "h0", "hq0": "g7"}
 FUSED = 640
-GATE_LOADS = ((1, 0, FUSED), (0, 0, T), (1, FUSED, T))
 
 
 def tile_moe_cap2_glu_gelu_kernel(
@@ -49,40 +49,40 @@ def tile_moe_cap2_glu_gelu_kernel(
         held = ctx.enter_context(tc.tile_pool(name="held", bufs=1))
         psum = ctx.enter_context(tc.psum_pool(name="psum", bufs=1))
 
-        offs_t = held.tile([P, S // 16], U16, name="offs_t")
-        pos1_t = held.tile([P, T // 16], U16, name="pos1_t")
-        pos2_t = held.tile([P, T // 16], U16, name="pos2_t")
+        def sbuf(name, shape, dtype):
+            return held.tile([P] + shape, dtype, name=TAG.get(name, name), align_bytes=ALIGN)
 
-        def zero(tile_3d):
-            nc.vector.memset(tile_3d.rearrange("p e n -> p (e n)").bitcast(I32), 0)
+        def zero(plane):
+            nc.vector.memset(plane.bitcast(I32), 0)
 
-        y = held.tile([P, S + PAD], F32, name="y")
-        zeros = held.tile([P, PAD], F32, name="zeros")
+        def group_of(groups, e):
+            return [g for g, grp in enumerate(groups) if grp[0] <= e < grp[1]][0]
+
+        offs_t = sbuf("offs_t", [S // 16], U16)
+        pos1_t = sbuf("pos1_t", [T // 16], U16)
+        pos2_t = sbuf("pos2_t", [T // 16], U16)
+
+        y = sbuf("y", [S + PAD], F32)
+        zeros = sbuf("zeros", [PAD], F32)
         nc.gpsimd.memset(zeros[:], 0.0)
         nc.scalar.activation(y[:, S:], zeros[:], GELU)
-        ident = held.tile([P, P], F32, name="ident")
+        ident = sbuf("ident", [P], F32)
         make_identity(nc, ident[:])
 
-        planes = {}
-        for i, g in [(i, g) for kind, i, g in LOADS if kind == "s"]:
-            e0, e1 = SCALE_GROUPS[i][g]
-            planes[i, g] = held.tile([P, e1 - e0, H], U8, name=f"plane{i}_{g}", align_bytes=256)
-            zero(planes[i, g][:])
-        s2 = held.tile([P, E, N], U8, name="s2", align_bytes=256)
-        xs = held.tile([P, T], U8, name="xs", align_bytes=256)
-        zero(s2[:])
-        nc.vector.memset(xs[:].bitcast(I32), 0)
-        w2t = held.tile([P, E, 2 * N], U8, name="w2t", align_bytes=256)
-        words = {}
-        for i in range(2):
-            for g, (e0, e1) in enumerate(WORD_GROUPS[i]):
-                words[i, g] = held.tile([P, e1 - e0, 2 * H], U8, name=f"words{i}_{g}", align_bytes=256)
-        raw = [held.tile([P, 2, t1 - t0], F32, name=f"raw{c}", align_bytes=256) for c, (half, t0, t1) in enumerate(X_LOADS)]
-
-        def load_x(c):
-            half, t0, t1 = X_LOADS[c]
-            rows = xT.rearrange("(p j) w -> p j w", j=4)
-            nc.sync.dma_start(out=raw[c][:], in_=rows[:, 2 * half : 2 * half + 2, t0:t1])
+        planes, words = {}, {}
+        for kind, i, g in LOADS:
+            if kind == "s":
+                e0, e1 = SCALE_GROUPS[i][g]
+                planes[i, g] = sbuf(f"plane{i}_{g}", [e1 - e0, H], U8)
+                zero(planes[i, g][:].rearrange("p e n -> p (e n)"))
+            else:
+                words[i, g] = sbuf(f"words{i}_{g}", [2, 2 * H], U8)
+        s2 = sbuf("s2", [E, N], U8)
+        xs = sbuf("xs", [T], U8)
+        zero(s2[:].rearrange("p e n -> p (e n)"))
+        zero(xs[:])
+        w2t = sbuf("w2t", [E, 2 * N], U8)
+        raw = [sbuf(f"raw{c}", [2, t1 - t0], F32) for c, (half, t0, t1) in enumerate(X_LOADS)]
 
         def load_scales(plane, scales, e0, e1):
             for r in range(4):
@@ -91,34 +91,31 @@ def tile_moe_cap2_glu_gelu_kernel(
                     in_=scales.bitcast(I32)[e0:e1].rearrange("e s (q r) n -> r q (e s) n", r=4)[r],
                 )
 
-        def load_plane(i, g):
-            load_scales(planes[i, g], (w1_scales, w3_scales)[i], *SCALE_GROUPS[i][g])
+        def load_words(tile, src, e0, e1):
+            nc.sync.dma_start(out=tile[:].bitcast(I32), in_=src.bitcast(I32)[e0:e1].rearrange("e s p n -> p (e s) n"))
 
-        def load_words(i, g):
-            e0, e1 = WORD_GROUPS[i][g]
-            nc.sync.dma_start(
-                out=words[i, g][:].bitcast(I32),
-                in_=(w1_words, w3_words)[i].bitcast(I32)[e0:e1].rearrange("e s p n -> p (e s) n"),
-            )
-
-        for c in range(len(X_LOADS)):
-            load_x(c)
+        rows = xT.rearrange("(p j) w -> p j w", j=4)
+        for c, (half, t0, t1) in enumerate(X_LOADS):
+            nc.sync.dma_start(out=raw[c][:], in_=rows[:, 2 * half : 2 * half + 2, t0:t1])
         nc.sync.dma_start(offs_t[:], offs)
         for kind, i, g in LOADS:
-            (load_plane if kind == "s" else load_words)(i, g)
-        nc.sync.dma_start(out=w2t[:].bitcast(I32), in_=w2_words.bitcast(I32).rearrange("e s p n -> p (e s) n"))
+            if kind == "s":
+                load_scales(planes[i, g], (w1_scales, w3_scales)[i], *SCALE_GROUPS[i][g])
+            else:
+                load_words(words[i, g], (w1_words, w3_words)[i], *PAIRS[g])
+        load_words(w2t, w2_words, 0, E)
         load_scales(s2, w2_scales, 0, E)
         nc.sync.dma_start(pos1_t[:], pos1)
         nc.sync.dma_start(pos2_t[:], pos2)
-        gates = {}
-        for i, lo, hi in GATE_LOADS:
-            piece = held.tile([P, hi - lo], F32, name=f"gate{i}_{lo}", align_bytes=256)
-            nc.sync.dma_start(out=piece[:], in_=gate[i, :, lo:hi])
-            for t in range(lo, hi, P):
-                gates[i, t] = (piece, lo)
+        gate_second = sbuf("gate_second", [FUSED], F32)
+        gate_first = sbuf("gate_first", [FUSED], F32)
+        gate_both = sbuf("gate_both", [2, T - FUSED], F32)
+        nc.sync.dma_start(out=gate_second[:], in_=gate[1, :, :FUSED])
+        nc.sync.dma_start(out=gate_first[:], in_=gate[0, :, :FUSED])
+        nc.sync.dma_start(out=gate_both[:], in_=gate[:, :, FUSED:].rearrange("i p t -> p i t"))
 
-        xq = held.tile([P, T], U32, name="xq", align_bytes=256)
-        xb = [held.tile([P, t1 - t0, 4], BF16, name=f"xb{b}", align_bytes=256) for b, (t0, t1) in enumerate(X_BLOCKS)]
+        xq = sbuf("xq", [T], U32)
+        xb = [sbuf(f"xb{b}", [t1 - t0, 4], BF16) for b, (t0, t1) in enumerate(X_BLOCKS)]
         for c, (half, t0, t1) in enumerate(X_LOADS):
             for b, (b0, b1) in enumerate(X_BLOCKS):
                 if b0 < t0 or b1 > t1:
@@ -135,34 +132,25 @@ def tile_moe_cap2_glu_gelu_kernel(
                 out=xq[:, b0:b1].bitcast(FP8X4), scales=xs[:, b0:b1], in_=xb[b][:].rearrange("p w j -> p (w j)")
             )
 
-        gq, gs, a_t, b_t, g_t, h_t, hi_t, hq_t, hs_t, y_t = [{} for i in range(10)]
-
-        def group_of(groups, e):
-            return [g for g, grp in enumerate(groups) if grp[0] <= e < grp[1]][0]
-
-        def coded(g):
-            e0, e1 = QUANT_GROUPS[g][:2]
-            hq_t[g] = held.tile([P, (e1 - e0) * C], U32, name=TAG.get(f"hq{g}", f"hq{g}"), align_bytes=256)
-            hs_t[g] = held.tile([P, (e1 - e0) * C], U8, name=f"hs{g}", align_bytes=256)
+        gq, gs, sums, kept, g_t, h_t, hi_t, hq_t, hs_t, y_t = [{} for i in range(10)]
 
         def gather(g):
             e0, e1 = GATHER_GROUPS[g]
-            gq[g] = held.tile([P, (e1 - e0) * C], U32, name=TAG.get(f"gq{g}", f"gq{g}"), align_bytes=256)
-            gs[g] = held.tile([P, (e1 - e0) * C], U8, name=TAG.get(f"gs{g}", f"gs{g}"), align_bytes=256)
+            gq[g] = sbuf(f"gq{g}", [(e1 - e0) * C], U32)
+            gs[g] = sbuf(f"gs{g}", [(e1 - e0) * C], U8)
             lst = offs_t[:, e0 * C // 16 : e1 * C // 16]
             nc.vector.tensor_copy(gq[g][:], xq[:].indirect(lst))
             nc.vector.tensor_copy(gs[g][:], xs[:].indirect(lst))
 
         def first(i, e):
-            g, s, w = group_of(GATHER_GROUPS, e), group_of(SCALE_GROUPS[i], e), group_of(WORD_GROUPS[i], e)
+            g, s = group_of(GATHER_GROUPS, e), group_of(SCALE_GROUPS[i], e)
             slots = slice((e - GATHER_GROUPS[g][0]) * C, (e - GATHER_GROUPS[g][0] + 1) * C)
-            acc = psum.tile([P, H], F32, name=f"bank{(A_BANKS, B_BANKS)[i][e]}")
-            (a_t, b_t)[i][e] = acc
+            sums[i, e] = psum.tile([P, H], F32, name=f"bank{BANKS[i][e]}")
             nc.tensor.matmul_mx(
-                out=acc[:],
+                out=sums[i, e][:],
                 lhsT=gq[g][:, slots].bitcast(FP8X4),
                 lhsT_scale=gs[g][:, slots],
-                rhs=words[i, w][:, e - WORD_GROUPS[i][w][0]].bitcast(FP4X4),
+                rhs=words[i, e // 2][:, e % 2].bitcast(FP4X4),
                 rhs_scale=planes[i, s][:, e - SCALE_GROUPS[i][s][0]],
                 start=True,
                 stop=True,
@@ -172,140 +160,125 @@ def tile_moe_cap2_glu_gelu_kernel(
             return acc[:].rearrange("s (p u w) -> s u p w", u=2, w=2)
 
         def gelu(e):
-            g_t[e] = held.tile([P, 2, P, 2], F32, name=f"g{e}", align_bytes=256)
-            nc.scalar.activation(g_t[e][:], by_pairs(a_t[e]), GELU)
+            first(W1, e)
+            g_t[e] = sbuf(f"g{e}", [2, P, 2], F32)
+            nc.scalar.activation(g_t[e][:], by_pairs(sums[W1, e]), GELU)
 
-        def spill(e):
-            kept = held.tile([P, 2, P, 2], F32, name=f"kept{e}", align_bytes=256)
-            nc.scalar.copy(kept[:], by_pairs(b_t[e]))
-            b_t[e] = kept
+        def gated_sums(e):
+            first(W3, e)
+            if e in ON_GPSIMD:
+                kept[e] = sbuf(f"kept{e}", [2, P, 2], F32)
+                nc.scalar.copy(kept[e][:], by_pairs(sums[W3, e]))
 
-        def mul(e):
-            h_t[e] = held.tile([P, 2, P, 2], BF16, name=TAG.get(f"h{e}", f"h{e}"), align_bytes=256)
+        def product(e):
+            h_t[e] = sbuf(f"h{e}", [2, P, 2], BF16)
             if e in ON_GPSIMD:
                 flat = "s u p w -> s (u p w)"
-                nc.gpsimd.tensor_tensor(
-                    h_t[e][:].rearrange(flat), b_t[e][:].rearrange(flat), g_t[e][:].rearrange(flat), MULT
-                )
+                nc.gpsimd.tensor_tensor(h_t[e][:].rearrange(flat), kept[e][:].rearrange(flat), g_t[e][:].rearrange(flat), MULT)
             elif e == E - 1:
                 for u in range(2):
-                    nc.vector.tensor_tensor(h_t[e][:, u], by_pairs(b_t[e])[:, u], g_t[e][:, u], MULT)
+                    nc.vector.tensor_tensor(h_t[e][:, u], by_pairs(sums[W3, e])[:, u], g_t[e][:, u], MULT)
             else:
-                nc.vector.tensor_tensor(h_t[e][:], by_pairs(b_t[e]), g_t[e][:], MULT)
+                nc.vector.tensor_tensor(h_t[e][:], by_pairs(sums[W3, e]), g_t[e][:], MULT)
 
-        def turn(e0, e1, bank):
-            xt = psum.tile([P, e1 - e0, 2, P], F32, name=f"bank{bank}")
-            for e in range(e0, e1):
+        def coded_place(e):
+            g = [g for g, grp in enumerate(QUANT_GROUPS) if e in grp][0]
+            return g, QUANT_GROUPS[g].index(e) * C
+
+        def turn(experts, bank):
+            xt = psum.tile([P, len(experts), 2, P], F32, name=f"bank{bank}")
+            for j, e in enumerate(experts):
                 pairs = h_t[e][:].rearrange("s u p w -> s (u p w)").bitcast(F32)
                 for u in range(2):
-                    nc.tensor.transpose(xt[:, e - e0, u], pairs[:, u * P : (u + 1) * P], ident[:])
-            g = group_of(QUANT_GROUPS, e0)
-            q0, q1 = QUANT_GROUPS[g][:2]
+                    nc.tensor.transpose(xt[:, j, u], pairs[:, u * P : (u + 1) * P], ident[:])
+            g, col = coded_place(experts[0])
             if g not in hi_t:
-                hi_t[g] = held.tile([P, (q1 - q0) * C * 4], BF16, name=TAG.get(f"hi{g}", f"hi{g}"), align_bytes=256)
-            mine = hi_t[g][:, (e0 - q0) * C * 4 : (e1 - q0) * C * 4]
+                hi_t[g] = sbuf(f"hi{g}", [len(QUANT_GROUPS[g]) * C * 4], BF16)
+            mine = hi_t[g][:, col * 4 : (col + len(experts) * C) * 4]
             nc.scalar.copy(
                 mine.bitcast(F32).rearrange("p (e s u) -> p e s u", s=C, u=2), xt[:].rearrange("p e u s -> p e s u")
             )
 
         def quant(g):
-            coded(g)
+            hq_t[g] = sbuf(f"hq{g}", [len(QUANT_GROUPS[g]) * C], U32)
+            hs_t[g] = sbuf(f"hs{g}", [len(QUANT_GROUPS[g]) * C], U8)
             nc.vector.quantize_mx(out=hq_t[g][:].bitcast(FP8X4), scales=hs_t[g][:], in_=hi_t[g][:])
 
         def second(k):
-            e0, e1, bank = KEEP_GROUPS[k]
-            y_t[k] = psum.tile([P, (e1 - e0) * C], F32, name=f"bank{bank}")
-            for e in range(e0, e1):
-                g = group_of(QUANT_GROUPS, e)
-                cols = slice((e - QUANT_GROUPS[g][0]) * C, (e - QUANT_GROUPS[g][0] + 1) * C)
+            experts, bank = KEEP_GROUPS[k]
+            y_t[k] = psum.tile([P, len(experts), C], F32, name=f"bank{bank}")
+            for j, e in enumerate(experts):
+                g, col = coded_place(e)
                 nc.tensor.matmul_mx(
-                    out=y_t[k][:, (e - e0) * C : (e - e0 + 1) * C],
+                    out=y_t[k][:, j],
                     lhsT=w2t[:, e].bitcast(FP4X4),
                     lhsT_scale=s2[:, e],
-                    rhs=hq_t[g][:, cols].bitcast(FP8X4),
-                    rhs_scale=hs_t[g][:, cols],
+                    rhs=hq_t[g][:, col : col + C].bitcast(FP8X4),
+                    rhs_scale=hs_t[g][:, col : col + C],
                     start=True,
                     stop=True,
                 )
 
         def keep(k):
-            e0, e1 = KEEP_GROUPS[k][:2]
+            experts = KEEP_GROUPS[k][0]
             copy = nc.vector.tensor_copy if k in KEEP_ON_VECTOR else nc.scalar.copy
-            copy(y[:, e0 * C : e1 * C], y_t[k][:])
+            if len(experts) == 1:
+                copy(y[:, experts[0] * C : (experts[0] + 1) * C], y_t[k][:, 0])
+            else:
+                run = len(experts) // 2
+                threes = y[:, : 6 * C].rearrange("p (a c) -> p a c", a=2)
+                copy(threes[:, :, experts[0] * C : (experts[0] + run) * C], y_t[k][:].rearrange("p (a e) c -> p a (e c)", a=2))
 
-        def gate_of(e):
-            first(0, e)
-            gelu(e)
-
-        def product_of(e):
-            first(1, e)
-            if e in ON_GPSIMD:
-                spill(e)
-            mul(e)
-
-        def pair(e0):
-            for step in (gate_of, product_of):
-                for e in (e0, e0 + 1):
+        def pair(j, steps):
+            for step in steps:
+                for e in range(*PAIRS[j]):
                     step(e)
 
         for g in range(3):
             gather(g)
-        pair(0)
+        pair(0, (gelu, gated_sums, product))
         gather(3)
-        gate_of(2)
-        gate_of(3)
-        first(1, 2)
-        spill(2)
-        first(1, 3)
-        turn(*TURN_GROUPS[0])
+        pair(1, (gelu, gated_sums))
+        turn(*TURNS[0])
         gather(4)
-        mul(2)
-        mul(3)
-        for e0 in (4, 6):
-            pair(e0)
-        for grp in TURN_GROUPS[1:]:
+        pair(1, (product,))
+        for j in (2, 3):
+            pair(j, (gelu, gated_sums, product))
+        for grp in TURNS[1:]:
             turn(*grp)
         for g in range(len(QUANT_GROUPS)):
             quant(g)
-        for k in range(len(KEEP_GROUPS)):
-            second(k)
-        for k in range(len(KEEP_GROUPS)):
-            keep(k)
+        for step in (second, keep):
+            for k in range(len(KEEP_GROUPS)):
+                step(k)
 
-        lists = (pos1_t, pos2_t)
-        picked = [held.tile([P, T], F32, name="picked0"), held.tile([P, T - FUSED], F32, name="picked1")]
-        weighted = [held.tile([P, T], F32, name=f"weighted{i}") for i in range(2)]
+        picked = sbuf("picked", [T + T - FUSED], F32)
+        weighted = [sbuf("weighted0", [FUSED], F32), sbuf("weighted1", [FUSED], F32)]
+        both = sbuf("both", [2 * (T - FUSED)], F32)
 
-        def gate_of_tokens(i, lo, hi):
-            tile, start = gates[i, lo]
-            return tile[:, lo - start : hi - start]
+        def fetch(lst, lo, hi, at):
+            nc.scalar.activation(picked[:, at : at + hi - lo], y[:].indirect(lst[:, lo // 16 : hi // 16]), COPY)
 
-        def results(i, lo, hi):
-            return y[:].indirect(lists[i][:, lo // 16 : hi // 16])
+        def weigh(lo, hi):
+            nc.vector.tensor_tensor(weighted[0][:, lo:hi], picked[:, lo:hi], gate_first[:, lo:hi], MULT)
 
-        def fetched(i, lo, hi):
-            return picked[i][:, lo - i * FUSED : hi - i * FUSED]
-
-        def fetch(i, lo, hi):
-            nc.scalar.activation(fetched(i, lo, hi), results(i, lo, hi), COPY)
-
-        def weigh(i, lo, hi):
-            nc.vector.tensor_tensor(weighted[i][:, lo:hi], fetched(i, lo, hi), gate_of_tokens(i, lo, hi), MULT)
-
-        def finish(lo, hi):
-            total = held.tile([P, hi - lo], F32, name=f"total{lo}", align_bytes=256)
-            nc.vector.tensor_tensor(total[:], weighted[0][:, lo:hi], weighted[1][:, lo:hi], ADD)
+        def finish(lo, hi, one, other):
+            total = sbuf(f"total{lo}", [hi - lo], F32)
+            nc.vector.tensor_tensor(total[:], one, other, ADD)
             nc.sync.dma_start(out=out[:, lo:hi], in_=total[:])
 
+        def finish_fused(lo, hi):
+            finish(lo, hi, weighted[0][:, lo:hi], weighted[1][:, lo:hi])
+
         for lo in (0, 256, 512):
-            fetch(0, lo, lo + 256)
-        fetch(1, FUSED, T)
-        nc.vector.tensor_tensor(weighted[1][:, :FUSED], results(1, 0, FUSED), gate_of_tokens(1, 0, FUSED), MULT)
-        weigh(0, 0, 256)
-        weigh(0, 256, 512)
-        finish(0, 256)
-        finish(256, 512)
-        weigh(0, 512, T)
-        weigh(1, FUSED, T)
-        finish(512, FUSED)
-        finish(FUSED, T)
+            fetch(pos1_t, lo, lo + 256, lo)
+        fetch(pos2_t, FUSED, T, T)
+        nc.vector.tensor_tensor(weighted[1][:], y[:].indirect(pos2_t[:, : FUSED // 16]), gate_second[:], MULT)
+        weigh(0, 256)
+        weigh(256, 512)
+        finish_fused(0, 256)
+        weigh(512, FUSED)
+        finish_fused(256, 512)
+        nc.vector.tensor_tensor(both[:], picked[:, FUSED:], gate_both[:].rearrange("p i t -> p (i t)"), MULT)
+        finish_fused(512, FUSED)
+        finish(FUSED, T, both[:, : T - FUSED], both[:, T - FUSED :])

@@ -37,7 +37,7 @@ TURNS = (((0, 1), 2), ((3, 4), 2), ((5, 2), 3), ((6,), 1), ((7,), 0))
 QUANT_GROUPS = ((0, 1), (3, 4), (5, 2), (6,), (7,))
 KEEP_GROUPS = (((0, 1, 3, 4), 4), ((2, 5), 5), ((6,), 6), ((7,), 7))
 KEEP_ON_VECTOR = (0, 2)
-TAG = {"h2": "xq", "gs3": "g0", "gq4": "g1", "gs4": "h0", "hq0": "g7"}
+TAG = {"h2": "xs", "gs3": "g0", "gq4": "g1", "gs4": "h0", "hq0": "g7"}
 FUSED = 640
 
 

from contextlib import ExitStack

import concourse.mybir as mybir
from concourse.masks import make_identity

K, T, E, C, H, N = 512, 768, 8, 128, 512, 128
PAD = 32
P = 128
S = E * C
FLOPS = 2 * S * (2 * K * H + H * N)

F32 = mybir.dt.float32
BF16 = mybir.dt.bfloat16
I32 = mybir.dt.int32
U32 = mybir.dt.uint32
U16 = mybir.dt.uint16
U8 = mybir.dt.uint8
FP8X4 = mybir.dt.float8_e4m3fn_x4
FP4X4 = mybir.dt.float4_e2m1fn_x4
GELU = mybir.ActivationFunctionType.Gelu_apprx_tanh
MULT = mybir.AluOpType.mult
ADD = mybir.AluOpType.add
COPY = mybir.ActivationFunctionType.Copy

ALIGN = 256
X_LOADS = ((0, 0, T), (1, 0, 512), (1, 512, T))
X_BLOCKS = ((0, 256), (256, 512), (512, T))
X_ON_VECTOR = ((256, 256, 0), (256, 48, 128))
W1, W3 = 0, 1
SCALE_GROUPS = (((0, 4), (4, 8)), ((0, 8),))
PAIRS = ((0, 2), (2, 4), (4, 6), (6, 8))
LOADS = (("s", W1, 0), ("w", W1, 0), ("w", W3, 0), ("s", W3, 0), ("w", W1, 1), ("w", W3, 1), ("s", W1, 1), ("w", W1, 2), ("w", W3, 2), ("w", W1, 3), ("w", W3, 3))
GATHER_GROUPS = ((0, 1), (1, 2), (2, 4), (4, 6), (6, 8))
ON_GPSIMD = (2,)
BANKS = ((0, 1, 2, 3, 0, 1, 2, 3), (4, 5, 6, 7, 4, 5, 6, 7))
TURNS = (((0, 1), 2), ((3, 4), 2), ((5, 2), 3), ((6,), 1), ((7,), 0))
QUANT_GROUPS = ((0, 1), (3, 4), (5, 2), (6,), (7,))
KEEP_GROUPS = (((0, 1, 3, 4), 4), ((2, 5), 5), ((6,), 6), ((7,), 7))
KEEP_ON_VECTOR = (0, 2)
TAG = {"h2": "xs", "gs3": "g0", "gq4": "g1", "gs4": "h0", "hq0": "g7"}
FUSED = 640


def tile_moe_cap2_glu_gelu_kernel(
    tc, xT, w1_words, w1_scales, w3_words, w3_scales, w2_words, w2_scales, gate, offs, pos1, pos2, out
):
    nc = tc.nc
    with ExitStack() as ctx:
        held = ctx.enter_context(tc.tile_pool(name="held", bufs=1))
        psum = ctx.enter_context(tc.psum_pool(name="psum", bufs=1))

        def sbuf(name, shape, dtype):
            return held.tile([P] + shape, dtype, name=TAG.get(name, name), align_bytes=ALIGN)

        def zero(plane):
            nc.vector.memset(plane.bitcast(I32), 0)

        def group_of(groups, e):
            return [g for g, grp in enumerate(groups) if grp[0] <= e < grp[1]][0]

        offs_t = sbuf("offs_t", [S // 16], U16)
        pos1_t = sbuf("pos1_t", [T // 16], U16)
        pos2_t = sbuf("pos2_t", [T // 16], U16)

        y = sbuf("y", [S + PAD], F32)
        zeros = sbuf("zeros", [PAD], F32)
        nc.gpsimd.memset(zeros[:], 0.0)
        nc.scalar.activation(y[:, S:], zeros[:], GELU)
        ident = sbuf("ident", [P], F32)
        make_identity(nc, ident[:])

        planes, words = {}, {}
        for kind, i, g in LOADS:
            if kind == "s":
                e0, e1 = SCALE_GROUPS[i][g]
                planes[i, g] = sbuf(f"plane{i}_{g}", [e1 - e0, H], U8)
                zero(planes[i, g][:].rearrange("p e n -> p (e n)"))
            else:
                words[i, g] = sbuf(f"words{i}_{g}", [2, 2 * H], U8)
        s2 = sbuf("s2", [E, N], U8)
        xs = sbuf("xs", [T], U8)
        zero(s2[:].rearrange("p e n -> p (e n)"))
        zero(xs[:])
        w2t = sbuf("w2t", [E, 2 * N], U8)
        raw = [sbuf(f"raw{c}", [2, t1 - t0], F32) for c, (half, t0, t1) in enumerate(X_LOADS)]

        def load_scales(plane, scales, e0, e1):
            for r in range(4):
                nc.sync.dma_start(
                    out=plane[r:P:32].bitcast(I32),
                    in_=scales.bitcast(I32)[e0:e1].rearrange("e s (q r) n -> r q (e s) n", r=4)[r],
                )

        def load_words(tile, src, e0, e1):
            nc.sync.dma_start(out=tile[:].bitcast(I32), in_=src.bitcast(I32)[e0:e1].rearrange("e s p n -> p (e s) n"))

        rows = xT.rearrange("(p j) w -> p j w", j=4)
        for c, (half, t0, t1) in enumerate(X_LOADS):
            nc.sync.dma_start(out=raw[c][:], in_=rows[:, 2 * half : 2 * half + 2, t0:t1])
        nc.sync.dma_start(offs_t[:], offs)
        for kind, i, g in LOADS:
            if kind == "s":
                load_scales(planes[i, g], (w1_scales, w3_scales)[i], *SCALE_GROUPS[i][g])
            else:
                load_words(words[i, g], (w1_words, w3_words)[i], *PAIRS[g])
        load_words(w2t, w2_words, 0, E)
        load_scales(s2, w2_scales, 0, E)
        nc.sync.dma_start(pos1_t[:], pos1)
        nc.sync.dma_start(pos2_t[:], pos2)
        gate_second = sbuf("gate_second", [FUSED], F32)
        gate_first = sbuf("gate_first", [FUSED], F32)
        gate_both = sbuf("gate_both", [2, T - FUSED], F32)
        nc.sync.dma_start(out=gate_second[:], in_=gate[1, :, :FUSED])
        nc.sync.dma_start(out=gate_first[:], in_=gate[0, :, :FUSED])
        nc.sync.dma_start(out=gate_both[:], in_=gate[:, :, FUSED:].rearrange("i p t -> p i t"))

        xq = sbuf("xq", [T], U32)
        xb = [sbuf(f"xb{b}", [t1 - t0, 4], BF16) for b, (t0, t1) in enumerate(X_BLOCKS)]
        for c, (half, t0, t1) in enumerate(X_LOADS):
            for b, (b0, b1) in enumerate(X_BLOCKS):
                if b0 < t0 or b1 > t1:
                    continue
                share = X_ON_VECTOR[half][b]
                src = raw[c][:, :, b0 - t0 : b1 - t0].rearrange("p j (q i) -> p q j i", i=4)
                dst = xb[b][:, :, 2 * half : 2 * half + 2].rearrange("p (q i) j -> p q j i", i=4)
                if share > 0:
                    nc.vector.tensor_copy(out=dst[:, : share // 4], in_=src[:, : share // 4])
                if share < b1 - b0:
                    nc.scalar.copy(out=dst[:, share // 4 :], in_=src[:, share // 4 :])
        for b, (b0, b1) in enumerate(X_BLOCKS):
            nc.vector.quantize_mx(
                out=xq[:, b0:b1].bitcast(FP8X4), scales=xs[:, b0:b1], in_=xb[b][:].rearrange("p w j -> p (w j)")
            )

        gq, gs, sums, kept, g_t, h_t, hi_t, hq_t, hs_t, y_t = [{} for i in range(10)]

        def gather(g):
            e0, e1 = GATHER_GROUPS[g]
            gq[g] = sbuf(f"gq{g}", [(e1 - e0) * C], U32)
            gs[g] = sbuf(f"gs{g}", [(e1 - e0) * C], U8)
            lst = offs_t[:, e0 * C // 16 : e1 * C // 16]
            nc.vector.tensor_copy(gq[g][:], xq[:].indirect(lst))
            nc.vector.tensor_copy(gs[g][:], xs[:].indirect(lst))

        def first(i, e):
            g, s = group_of(GATHER_GROUPS, e), group_of(SCALE_GROUPS[i], e)
            slots = slice((e - GATHER_GROUPS[g][0]) * C, (e - GATHER_GROUPS[g][0] + 1) * C)
            sums[i, e] = psum.tile([P, H], F32, name=f"bank{BANKS[i][e]}")
            nc.tensor.matmul_mx(
                out=sums[i, e][:],
                lhsT=gq[g][:, slots].bitcast(FP8X4),
                lhsT_scale=gs[g][:, slots],
                rhs=words[i, e // 2][:, e % 2].bitcast(FP4X4),
                rhs_scale=planes[i, s][:, e - SCALE_GROUPS[i][s][0]],
                start=True,
                stop=True,
            )

        def by_pairs(acc):
            return acc[:].rearrange("s (p u w) -> s u p w", u=2, w=2)

        def gelu(e):
            first(W1, e)
            g_t[e] = sbuf(f"g{e}", [2, P, 2], F32)
            nc.scalar.activation(g_t[e][:], by_pairs(sums[W1, e]), GELU)

        def gated_sums(e):
            first(W3, e)
            if e in ON_GPSIMD:
                kept[e] = sbuf(f"kept{e}", [2, P, 2], F32)
                nc.scalar.copy(kept[e][:], by_pairs(sums[W3, e]))

        def product(e):
            h_t[e] = sbuf(f"h{e}", [2, P, 2], BF16)
            if e in ON_GPSIMD:
                flat = "s u p w -> s (u p w)"
                nc.gpsimd.tensor_tensor(h_t[e][:].rearrange(flat), kept[e][:].rearrange(flat), g_t[e][:].rearrange(flat), MULT)
            elif e == E - 1:
                for u in range(2):
                    nc.vector.tensor_tensor(h_t[e][:, u], by_pairs(sums[W3, e])[:, u], g_t[e][:, u], MULT)
            else:
                nc.vector.tensor_tensor(h_t[e][:], by_pairs(sums[W3, e]), g_t[e][:], MULT)

        def coded_place(e):
            g = [g for g, grp in enumerate(QUANT_GROUPS) if e in grp][0]
            return g, QUANT_GROUPS[g].index(e) * C

        def turn(experts, bank):
            xt = psum.tile([P, len(experts), 2, P], F32, name=f"bank{bank}")
            for j, e in enumerate(experts):
                pairs = h_t[e][:].rearrange("s u p w -> s (u p w)").bitcast(F32)
                for u in range(2):
                    nc.tensor.transpose(xt[:, j, u], pairs[:, u * P : (u + 1) * P], ident[:])
            g, col = coded_place(experts[0])
            if g not in hi_t:
                hi_t[g] = sbuf(f"hi{g}", [len(QUANT_GROUPS[g]) * C * 4], BF16)
            mine = hi_t[g][:, col * 4 : (col + len(experts) * C) * 4]
            nc.scalar.copy(
                mine.bitcast(F32).rearrange("p (e s u) -> p e s u", s=C, u=2), xt[:].rearrange("p e u s -> p e s u")
            )

        def quant(g):
            hq_t[g] = sbuf(f"hq{g}", [len(QUANT_GROUPS[g]) * C], U32)
            hs_t[g] = sbuf(f"hs{g}", [len(QUANT_GROUPS[g]) * C], U8)
            nc.vector.quantize_mx(out=hq_t[g][:].bitcast(FP8X4), scales=hs_t[g][:], in_=hi_t[g][:])

        def second(k):
            experts, bank = KEEP_GROUPS[k]
            y_t[k] = psum.tile([P, len(experts), C], F32, name=f"bank{bank}")
            for j, e in enumerate(experts):
                g, col = coded_place(e)
                nc.tensor.matmul_mx(
                    out=y_t[k][:, j],
                    lhsT=w2t[:, e].bitcast(FP4X4),
                    lhsT_scale=s2[:, e],
                    rhs=hq_t[g][:, col : col + C].bitcast(FP8X4),
                    rhs_scale=hs_t[g][:, col : col + C],
                    start=True,
                    stop=True,
                )

        def keep(k):
            experts = KEEP_GROUPS[k][0]
            copy = nc.vector.tensor_copy if k in KEEP_ON_VECTOR else nc.scalar.copy
            if len(experts) == 1:
                copy(y[:, experts[0] * C : (experts[0] + 1) * C], y_t[k][:, 0])
            else:
                run = len(experts) // 2
                threes = y[:, : 6 * C].rearrange("p (a c) -> p a c", a=2)
                copy(threes[:, :, experts[0] * C : (experts[0] + run) * C], y_t[k][:].rearrange("p (a e) c -> p a (e c)", a=2))

        def pair(j, steps):
            for step in steps:
                for e in range(*PAIRS[j]):
                    step(e)

        for g in range(3):
            gather(g)
        pair(0, (gelu, gated_sums, product))
        gather(3)
        pair(1, (gelu, gated_sums))
        turn(*TURNS[0])
        gather(4)
        pair(1, (product,))
        for j in (2, 3):
            pair(j, (gelu, gated_sums, product))
        for grp in TURNS[1:]:
            turn(*grp)
        for g in range(len(QUANT_GROUPS)):
            quant(g)
        for step in (second, keep):
            for k in range(len(KEEP_GROUPS)):
                step(k)

        picked = sbuf("picked", [T + T - FUSED], F32)
        weighted = [sbuf("weighted0", [FUSED], F32), sbuf("weighted1", [FUSED], F32)]
        both = sbuf("both", [2 * (T - FUSED)], F32)

        def fetch(lst, lo, hi, at):
            nc.scalar.activation(picked[:, at : at + hi - lo], y[:].indirect(lst[:, lo // 16 : hi // 16]), COPY)

        def weigh(lo, hi):
            nc.vector.tensor_tensor(weighted[0][:, lo:hi], picked[:, lo:hi], gate_first[:, lo:hi], MULT)

        def finish(lo, hi, one, other):
            total = sbuf(f"total{lo}", [hi - lo], F32)
            nc.vector.tensor_tensor(total[:], one, other, ADD)
            nc.sync.dma_start(out=out[:, lo:hi], in_=total[:])

        def finish_fused(lo, hi):
            finish(lo, hi, weighted[0][:, lo:hi], weighted[1][:, lo:hi])

        for lo in (0, 256, 512):
            fetch(pos1_t, lo, lo + 256, lo)
        fetch(pos2_t, FUSED, T, T)
        nc.vector.tensor_tensor(weighted[1][:], y[:].indirect(pos2_t[:, : FUSED // 16]), gate_second[:], MULT)
        weigh(0, 256)
        weigh(256, 512)
        finish_fused(0, 256)
        weigh(512, FUSED)
        finish_fused(256, 512)
        nc.vector.tensor_tensor(both[:], picked[:, FUSED:], gate_both[:].rearrange("p i t -> p (i t)"), MULT)
        finish_fused(512, FUSED)
        finish(FUSED, T, both[:, : T - FUSED], both[:, T - FUSED :])
